import numpy as np
import ml_dtypes


def mxq(x, axis, fmt="e4m3"):
    dtype, down = {"e4m3": (ml_dtypes.float8_e4m3fn, 7), "e5m2": (ml_dtypes.float8_e5m2, 14)}[fmt]
    v = np.moveaxis(np.asarray(x, np.float32).astype(ml_dtypes.bfloat16).astype(np.float64), axis, -1)
    blocks = v.reshape(v.shape[:-1] + (-1, 32))
    amax = np.abs(blocks).max(-1, keepdims=True)
    byte = np.maximum(np.where(amax > 0, np.frexp(amax)[1] - 1 + 127, 0) - down, 1)
    scale = np.exp2(byte - 127.0)
    codes = (blocks / scale).astype(np.float32).astype(dtype).astype(np.float64)
    return np.moveaxis((codes * scale).reshape(v.shape), -1, axis)


WIDE = False


def mx_kscale(k):
    if not WIDE:
        return np.ones(k)
    levels = np.array([10, -10, 5, -5, 0])
    if k % 512:
        return np.exp2(np.random.permutation(np.resize(levels, k // 32))).repeat(32)
    a = np.empty((k // 512, 16))
    for p in range(k // 512):
        a[p, :8] = np.random.permutation(np.resize(levels, 8))
        for g in range(8):
            far = levels[np.abs(levels - a[p, g]) >= 10]
            a[p, g + 8] = far[np.random.randint(len(far))]
    return np.exp2(a.ravel()).repeat(32)


BF16 = ml_dtypes.bfloat16


def bf(x):
    return np.asarray(x, np.float32).astype(BF16)


def f64(x):
    return np.asarray(x).astype(np.float64)


E2M1 = np.array([0.0, 0.5, 1.0, 1.5, 2.0, 3.0, 4.0, 6.0, -0.0, -0.5, -1.0, -1.5, -2.0, -3.0, -4.0, -6.0])


def pack_weight(w, fmt):
    k, n = w.shape
    w = f64(bf(w)).reshape(k // 32, 32, n)
    amax = np.abs(w).max(1)
    if fmt == "e4m3":
        byte = np.frexp(amax)[1] - 1 + 127 - 7
    else:
        mant, ex = np.frexp(amax / 6.0)
        byte = np.where(mant > 0.5, ex, ex - 1) + 127
    byte = np.clip(np.where(amax > 0, byte, 1), 1, 254)
    scaled = (w * np.exp2(127.0 - byte)[:, None, :]).reshape(k, n).astype(np.float32)
    by_word = np.ascontiguousarray(scaled.reshape(k // 512, 128, 4, n).transpose(0, 1, 3, 2))
    if fmt == "e4m3":
        words = by_word.astype(ml_dtypes.float8_e4m3fn).view(np.uint8)
    else:
        c = by_word.astype(ml_dtypes.float4_e2m1fn).view(np.uint8) & 0xF
        words = c[..., 0::2] | (c[..., 1::2] << 4)
    return np.ascontiguousarray(words), np.ascontiguousarray(byte.astype(np.uint8).reshape(k // 512, 16, n))


def unpack_weight(words, scales, fmt):
    g, p, n, _ = words.shape
    if fmt == "e4m3":
        vals = np.ascontiguousarray(words).view(ml_dtypes.float8_e4m3fn).astype(np.float64)
    else:
        nib = np.empty((g, p, n, 4), np.uint8)
        nib[..., 0::2] = words & 0xF
        nib[..., 1::2] = words >> 4
        vals = E2M1[nib]
    vals = vals * np.repeat(np.exp2(scales.astype(np.float64) - 127.0), 8, axis=1)[..., None]
    return vals.transpose(0, 1, 3, 2).reshape(g * 512, n)
def pack4(w):
    words, scales = pack_weight(w, "e2m1")
    return words.reshape(words.shape[0], 128, -1), scales


def unpack4(words, scales):
    return unpack_weight(words.reshape(words.shape[0], 128, -1, 2), scales, "e2m1")


M, K, D, C, R = 1024, 512, 2048, 512, 512


def setup_inputs():
    s, t, u = mx_kscale(K), mx_kscale(D), mx_kscale(M)
    rel = np.random.uniform(0.5, 1.5, K) / np.sqrt(K)
    sign1 = np.sign(np.random.standard_normal((K, D)))
    sign2 = np.sign(np.random.standard_normal((K, D)))
    v = np.random.standard_normal((D, C)) / np.sqrt(D)
    v_words, v_scales = pack4(v / t[:, None])
    return {"x": bf(np.random.standard_normal((M, K)) * s),
            "w1": bf(sign1 * (rel / s)[:, None]),
            "w2": bf(sign2 * (rel / s)[:, None]),
            "c": bf((1 + 0.1 * np.random.standard_normal(D)) * t),
            "r": bf(np.random.uniform(0.5, 1.5, M) * u),
            "v_words": v_words, "v_scales": v_scales,
            "y": bf(np.random.standard_normal((M, R)) / np.sqrt(M) / u[:, None])}


def reference(x, w1, w2, c, r, v_words, v_scales, y):
    xq = mxq(f64(x), 1, "e4m3")
    h1 = xq @ mxq(f64(w1), 0, "e4m3")
    h2 = xq @ mxq(f64(w2), 0, "e4m3")
    z = h1 * h2 * c.astype(np.float64) * f64(r)[:, None]
    pred = mxq(z, 1, "e4m3") @ unpack4(v_words, v_scales)
    moment = mxq(z, 0, "e4m3").T @ mxq(f64(y), 0, "e4m3")
    return pred, moment

@@ -1,0 +1,428 @@
+from contextlib import ExitStack
+
+import concourse.mybir as mybir
+from concourse.masks import make_identity
+
+M, K, D, C, R = 1024, 512, 2048, 512, 512
+FLOPS = 2 * (2 * M * K * D + M * D * C + M * D * R)
+
+F32 = mybir.dt.float32
+BF16 = mybir.dt.bfloat16
+U32 = mybir.dt.uint32
+I32 = mybir.dt.int32
+U8 = mybir.dt.uint8
+FP8X4 = mybir.dt.float8_e4m3fn_x4
+FP4X4 = mybir.dt.float4_e2m1fn_x4
+MULT = mybir.AluOpType.mult
+
+P = 128
+PASS = 512
+UNITS = [(0, 0), (0, 1), (1, 0), (1, 1), (2, 0), (3, 0), (2, 1), (3, 1)]
+HOLD = 3
+LENT = 0
+FEAT_QUANT_SLOT = 1
+GROUPS = (("zr", 0), ("zr", 1), ("zf", 0), ("zr", 2), ("zf", 1), ("zr", 3))
+DUE = {("w", 0, 1): 9, ("w", 1, 1): 17, ("y", 0, 0): 16, ("y", 1, 0): 19, ("w", 0, 2): 25, ("w", 1, 2): 33, ("w", 0, 3): 36, ("w", 1, 3): 41}
+V_Y = (11, 14)
+PRED_FROM = 40
+FIRST_PIECES = [2, 0, 1, 1, 1, 1, 1, 1]
+LAST_LENT = 0
+LATE_PASSES = [0, 0, 2, 2, 2, 2, 2, 1]
+LATE_FROM = 36
+RESULT_BUFS = 8
+H_BANKS = 3
+OUT_BANKS = 3
+PASSES_PER_SLOT = [0, 0, 1, 2, 1, 2, 1, 2]
+PIECES_PER_SLOT = [1, 0, 0, 1, 1, 2, 1, 2]
+ROWS_QUANT_SLOT = 5
+X1_SLOT = 1
+LATE_FEAT = {1: 50, 3: 52}
+LEND_TURN = 99
+V_HEAD = 2
+TAIL_FIRST = 8
+
+
+def take(queue):
+    first = queue[0]
+    queue[:] = queue[1:]
+    return first
+
+
+def tile_random_maclaurin_features_s8_kernel(tc, x, w1, w2, c, r, v_words, v_scales, y, out_0, out_1):
+    nc = tc.nc
+    n_slots = 8 * len(UNITS)
+    last_unit = len(UNITS) - 1
+
+    with ExitStack() as ctx:
+        keep = ctx.enter_context(tc.tile_pool(name="keep", bufs=1))
+        ring = ctx.enter_context(tc.tile_pool(name="ring", bufs=2))
+        psum = ctx.enter_context(tc.psum_pool(name="psum", bufs=1))
+        ctx.enter_context(tc.manual_schedule())
+
+        def bank(tag):
+            return psum.tile([P, PASS], F32, name=tag, tag=tag)
+
+        def mx_tiles(name):
+            codes = keep.tile([P, PASS], U32, name=name + "_codes", align_bytes=64)
+            scales = keep.tile([P, PASS], U8, name=name + "_scales", align_bytes=64)
+            return codes, scales
+
+        def quantize(mx, cols, src):
+            nc.vector.quantize_mx(out=mx[0][:, cols].bitcast(FP8X4), scales=mx[1][:, cols], in_=src)
+
+        def operand(mx, cols):
+            return mx[0][:, cols].bitcast(FP8X4), mx[1][:, cols]
+
+        def matmul(out, lhs, rhs, start, stop):
+            nc.tensor.matmul_mx(out=out, lhsT=lhs[0], lhsT_scale=lhs[1], rhs=rhs[0], rhs_scale=rhs[1], start=start, stop=stop)
+
+        whole = slice(0, PASS)
+
+        def quarter(i):
+            return slice(i * P, (i + 1) * P)
+
+        r_sb = keep.tile([P, 8], BF16, name="r_sb")
+        nc.scalar.dma_start(out=r_sb[:].rearrange("m (g t) -> m g t", g=2), in_=r.rearrange("(g m t) -> m g t", g=2, t=4))
+        c_sb = keep.tile([P, 16], BF16, name="c_sb")
+        nc.scalar.dma_start(out=c_sb[:].rearrange("m (f s) -> m f s", f=4), in_=c.rearrange("(f m s) -> m f s", f=4, s=4))
+
+        ident = keep.tile([P, P], F32, name="ident")
+        make_identity(nc, ident[:])
+        v_plane = keep.tile([P, 4 * C], U8, name="v_plane", align_bytes=64)
+        nc.gpsimd.memset(v_plane[:].bitcast(I32), 0)
+
+        raw = {}
+        x_rows = x.rearrange("(g m t) k -> g m (t k)", g=2, t=4)
+
+        def load_x(g):
+            for half in range(2):
+                tile = keep.tile([P, 2 * K], BF16, name="x_raw%d%d" % (g, half))
+                nc.sync.dma_start(out=tile[:], in_=x_rows[g][:, half * 2 * K : (half + 1) * 2 * K])
+                raw["x", g, half] = tile
+
+        def load_w(which, f):
+            tile = keep.tile([P, 4, PASS], BF16, name="w_raw%d%d" % (which, f))
+            src = (w1, w2)[which].rearrange("(p j) d -> p j d", j=4)
+            nc.sync.dma_start(out=tile[:], in_=src[:, :, f * PASS : (f + 1) * PASS])
+            raw["w", which, f] = tile
+
+        def load_w_half(half):
+            tile = keep.tile([P, 4, PASS // 2], BF16, name="w_first%d" % half)
+            src = w1.rearrange("(p j) d -> p j d", j=4)
+            nc.sync.dma_start(out=tile[:], in_=src[:, :, half * 256 : (half + 1) * 256])
+            raw["half", half] = tile
+
+        def load_y(g):
+            tile = keep.tile([P, 4, R], BF16, name="y_raw%d" % g)
+            nc.sync.dma_start(out=tile[:], in_=y.rearrange("(g p j) n -> g p j n", g=2, j=4)[g])
+            raw["y", g, 0] = tile
+
+        load_x(0)
+        load_w_half(0)
+        load_w_half(1)
+        load_w(1, 0)
+        load_x(1)
+        load_w(0, 1)
+        load_w(1, 1)
+        load_y(0)
+        load_y(1)
+        for f in (2, 3):
+            load_w(0, f)
+            load_w(1, f)
+        v_codes = keep.tile([P, 4, 2 * C], U8, name="v_codes", align_bytes=64)
+        nc.sync.dma_start(out=v_codes[:].bitcast(I32), in_=v_words.bitcast(I32).rearrange("f p n -> p f n"))
+        for q in range(4):
+            nc.sync.dma_start(
+                out=v_plane[:].bitcast(I32)[32 * q : 32 * q + 4, :].rearrange("p (f n) -> p f n", f=4),
+                in_=v_scales.bitcast(I32)[:, 4 * q : 4 * q + 4, :].rearrange("f p n -> p f n"),
+            )
+
+        staged = {}
+        mx = {}
+
+        def stage(key):
+            if key not in staged:
+                staged[key] = ring.tile([P, 4 * PASS], BF16, name="stage", tag="stage", bufs=5, align_bytes=64)
+            return staged[key]
+
+        def interleave(copy, key, lo, hi):
+            dst = stage(key)
+            if key[0] == "w":
+                copy(
+                    out=dst[:].rearrange("p (s a b j) -> p a s b j", s=4, b=2, j=4)[:, 16 * lo : 16 * hi],
+                    in_=raw[key][:].rearrange("p j (a b s) -> p a s b j", b=2, s=4)[:, 16 * lo : 16 * hi],
+                )
+            else:
+                copy(
+                    out=dst[:].rearrange("p (a i j) -> p a j i", i=4, j=4)[:, 32 * lo : 32 * hi],
+                    in_=raw[key][:].rearrange("p j (a i) -> p a j i", i=4)[:, 32 * lo : 32 * hi],
+                )
+
+        def quantize_staged(key):
+            mx[key] = mx_tiles("%s%d%d" % key)
+            quantize(mx[key], whole, staged[key][:])
+
+        def transpose_x(g, half, tag):
+            dst = bank(tag)
+            words = raw["x", g, half][:].bitcast(F32)
+            for t in range(2):
+                for u in range(2):
+                    nc.tensor.transpose(dst[:, quarter(2 * t + u)], words[:, 256 * t + u : 256 * (t + 1) : 2], ident[:])
+            return dst
+
+        def copy_x(g, half, src):
+            dst = stage(("x", g, 0))
+            nc.scalar.copy(
+                out=dst[:].bitcast(F32)[:, half * PASS : (half + 1) * PASS].rearrange("p (t m u) -> p t m u", t=2, u=2),
+                in_=src[:].rearrange("p (t u m) -> p t m u", t=2, u=2),
+            )
+
+        r_words = r_sb[:].bitcast(F32)
+        r_all = keep.tile([P, M], BF16, name="r_all")
+
+        def spread_r(g):
+            r_bank = bank("out%d" % g)
+            for h in range(2):
+                q = 2 * g + h
+                nc.tensor.transpose(r_bank[:, quarter(h)], r_words[:, q : q + 1].to_broadcast([P, P]), ident[:])
+            nc.scalar.copy(
+                out=r_all[:, g * PASS : (g + 1) * PASS].rearrange("p (h e m) -> p h e m", h=2, e=2),
+                in_=r_bank[:, 0 : 2 * P].bitcast(BF16).rearrange("p (h m e) -> p h e m", h=2, e=2),
+            )
+
+        spread_r(0)
+        spread_r(1)
+        x_banks = [transpose_x(0, half, "turn%d" % half) for half in range(2)]
+        for half in range(2):
+            copy_x(0, half, x_banks[half])
+        for half in range(2):
+            nc.vector.tensor_copy(
+                out=stage(("w", 0, 0))[:].rearrange("p (s a b j) -> p a s b j", s=4, b=2, j=4)[:, 32 * half : 32 * half + 32],
+                in_=raw["half", half][:].rearrange("p j (a b s) -> p a s b j", b=2, s=4),
+            )
+        mx["x", 0, 0] = mx_tiles("x00")
+        quantize(mx["x", 0, 0], slice(0, 256), staged["x", 0, 0][:, 0:1024])
+        quantize_staged(("w", 0, 0))
+        quantize(mx["x", 0, 0], slice(256, 512), staged["x", 0, 0][:, 1024:2048])
+        if V_HEAD:
+            interleave(nc.vector.tensor_copy, ("w", 1, 0), 0, V_HEAD)
+        interleave(nc.scalar.copy, ("w", 1, 0), V_HEAD, 4)
+
+        prep = [("w", 0, 1), ("w", 1, 1), ("y", 0, 0), ("y", 1, 0), ("w", 0, 2), ("w", 1, 2), ("w", 0, 3), ("w", 1, 3)]
+        pieces = [(key, i) for key in prep for i in range(4) if key != ("y", 0, 0) or not V_Y]
+        to_quantize = [(1, ("w", 1, 0)), (X1_SLOT + 3, ("x", 1, 0))]
+
+        h_bank = {}
+        scaled = {}
+        z_feat = {}
+        z_rows = {}
+        turned = {}
+        fresh = []
+        usable = set()
+
+        def fill(j):
+            u, i = divmod(j, 8)
+            f, g = UNITS[u]
+            dst = bank("h%d" % (j % H_BANKS))
+            h_bank[j] = dst
+            if i < 4:
+                matmul(dst[:], operand(mx["w", 0, f], quarter(i)), operand(mx["x", g, 0], whole), True, True)
+            else:
+                for s in range(4):
+                    matmul(dst[:, quarter(s)], operand(mx["w", 1, f], quarter(s)), operand(mx["x", g, 0], quarter(i - 4)), True, True)
+
+        def consume(j):
+            u, i = divmod(j, 8)
+            f, g = UNITS[u]
+            if i == 0:
+                scaled[u] = ring.tile([P, 4, PASS], F32, name="scaled", tag="scaled", bufs=2)
+                mx["zf", f, g] = mx_tiles("zf%d%d" % (f, g))
+            if i < 4:
+                nc.vector.scalar_tensor_tensor(
+                    out=scaled[u][:, i, :], in0=h_bank[j][:], scalar=c_sb[:, 4 * f + i : 4 * f + i + 1],
+                    in1=r_all[:, g * PASS : (g + 1) * PASS], op0=MULT, op1=MULT,
+                )
+                return
+            t = i - 4
+            if f == 3:
+                z_feat[u, t] = ring.tile([P, PASS], BF16, name="z_cell", tag="z_cell", bufs=8, align_bytes=64)
+            else:
+                if t == 0:
+                    z_feat[u, 4] = ring.tile([P, 4 * PASS], BF16, name="z_unit", tag="z_unit", bufs=4, align_bytes=64)
+                z_feat[u, t] = z_feat[u, 4][:, t * PASS : (t + 1) * PASS]
+            nc.vector.tensor_tensor(
+                out=z_feat[u, t][:].rearrange("p (n i s) -> p n s i", i=2, s=4),
+                in0=h_bank[j][:].rearrange("p (s n i) -> p n s i", s=4, i=2),
+                in1=scaled[u][:, :, quarter(t)].rearrange("p s (n i) -> p n s i", i=2),
+                op=MULT,
+            )
+
+        def quantize_feat(u, t):
+            f, g = UNITS[u]
+            quantize(mx["zf", f, g], quarter(t) if t < 4 else whole, z_feat[u, t][:])
+            for n in range(4):
+                if t in (n, 4):
+                    fresh.append(("zf", f, g, n))
+
+        def turn(u, cells=range(4)):
+            for h in range(2):
+                if (u, h) not in turned:
+                    turned[u, h] = bank("turn%d" % h)
+                for t in cells:
+                    nc.tensor.transpose(turned[u, h][:, quarter(t)], z_feat[u, t][:].bitcast(F32)[:, h : 256 : 2], ident[:])
+
+        def copy_turned(copy, u, h, lo, hi):
+            if (u, 0) not in z_rows:
+                z_rows[u, 0] = ring.tile([P, 4 * PASS], BF16, name="z_rows", tag="z_rows", bufs=2, align_bytes=64)
+            copy(
+                out=z_rows[u, 0][:].rearrange("m (p h e t) -> m h p e t", h=2, e=2, t=4)[:, h, lo:hi],
+                in_=turned[u, h][:].bitcast(BF16).rearrange("m (t p e) -> m p e t", t=4, e=2)[:, lo:hi],
+            )
+
+        def quantize_rows(u, lo, hi):
+            f, g = UNITS[u]
+            if ("zr", f, g) not in mx:
+                mx["zr", f, g] = mx_tiles("zr%d%d" % (f, g))
+            quantize(mx["zr", f, g], slice(4 * lo, 4 * hi), z_rows[u, 0][:, 16 * lo : 16 * hi])
+            for n in range(lo // 32, hi // 32):
+                fresh.append(("zr", f, g, n))
+
+        pred_rows = out_0.rearrange("(g m t) n -> g t m n", g=2, t=4)
+        moment_rows = out_1.rearrange("(f i m) n -> f i m n", f=4, i=4)
+        free_banks = ["out%d" % b for b in range(OUT_BANKS)]
+        finished = []
+        running = []
+        lent = []
+        clock = [0]
+        moments = [(moment_rows[f, i], [("zr", f, g, i) for g in range(2)]) for f in range(4) for i in range(4)]
+        preds = [(pred_rows[g, t], [("zf", f, g, t) for f in range(4)]) for g in range(2) for t in range(4)]
+
+        def open_group(banks, waiting):
+            tag = take(banks)
+            dram, passes = take(waiting)
+            group = dict(tag=tag, tile=bank(tag), dram=dram, passes=passes, done=0)
+            running.append(group)
+            return group
+
+        def pick():
+            for group in running:
+                if group["passes"][-1] in usable:
+                    return group
+            if moments and lent and moments[0][1][0] in usable:
+                return open_group(lent, moments)
+            if moments and free_banks and moments[0][1][-1] in usable:
+                return open_group(free_banks, moments)
+            for group in running:
+                if group["passes"][group["done"]] in usable:
+                    return group
+            if preds and clock[0] >= PRED_FROM and free_banks and preds[0][1][0] in usable and (len(running) < HOLD or preds[0][1][-1] in usable):
+                return open_group(free_banks, preds)
+            if moments and free_banks and not preds and moments[0][1][0] in usable:
+                return open_group(free_banks, moments)
+            return None
+
+        def one_pass():
+            group = pick()
+            if group is None:
+                return
+            n = group["done"]
+            total = len(group["passes"])
+            kind, f, g, i = group["passes"][n]
+            if kind == "zf":
+                rhs = (v_codes[:, f, :].bitcast(FP4X4), v_plane[:, f * C : (f + 1) * C])
+            else:
+                rhs = operand(mx["y", g, 0], whole)
+            matmul(group["tile"][:], operand(mx[kind, f, g], quarter(i)), rhs, n == 0, n == total - 1)
+            group["done"] = n + 1
+            if n == total - 1:
+                finished.append((group["tag"], group["tile"], group["dram"]))
+                running[:] = [other for other in running if other["tag"] != group["tag"]]
+
+        def run_passes(count):
+            while fresh:
+                usable.add(take(fresh))
+            for step in range(count):
+                one_pass()
+
+        def drain(copy):
+            tag, tile, dram = take(finished)
+            result = ring.tile([P, PASS], F32, name="result", tag="result", bufs=RESULT_BUFS)
+            copy(out=result[:], in_=tile[:])
+            nc.sync.dma_start(out=dram, in_=result[:])
+            if tag[0] != "t" or not open_units:
+                free_banks.append(tag)
+
+        open_units = [1]
+        ahead = H_BANKS - 1
+        for j in range(ahead):
+            fill(j)
+        for j in range(n_slots):
+            u, i = divmod(j, 8)
+            f, g = UNITS[u]
+            clock[0] = j
+            if i == 0 and u > 0:
+                assert not lent and all(group["tag"][0] != "t" for group in running)
+                turn(u - 1)
+            if j + ahead < n_slots:
+                fill(j + ahead)
+            if j == X1_SLOT:
+                x_banks = [transpose_x(1, half, "turn%d" % half) for half in range(2)]
+            if j >= 10:
+                run_passes((LATE_PASSES if j >= LATE_FROM else PASSES_PER_SLOT)[i])
+            consume(j)
+            for due, key in to_quantize:
+                if due == j:
+                    quantize_staged(key)
+            if j in V_Y:
+                half = V_Y.index(j)
+                interleave(nc.vector.tensor_copy, ("y", 0, 0), 2 * half, 2 * half + 2)
+                if half == 1:
+                    to_quantize.append((DUE["y", 0, 0], ("y", 0, 0)))
+            if i == FEAT_QUANT_SLOT and u > 0 and UNITS[u - 1][0] < 3 and u - 1 not in LATE_FEAT:
+                quantize_feat(u - 1, 4)
+            for late in LATE_FEAT:
+                if LATE_FEAT[late] == j + 1:
+                    quantize_feat(late, 4)
+            if i == 0 and u > 0 and UNITS[u - 1][0] == 3:
+                quantize_feat(u - 1, 3)
+            if f == 3 and i > 4:
+                quantize_feat(u, i - 5)
+            if i == ROWS_QUANT_SLOT and u > 0:
+                quantize_rows(u - 1, 0, P)
+            if j == X1_SLOT:
+                for half in range(2):
+                    copy_x(1, half, x_banks[half])
+            if i in (1, 2) and u > 0:
+                copy_turned(nc.scalar.copy, u - 1, i - 1, 0, P)
+            if i in (1, 2) and u > 0 and UNITS[u - 1][1] == 1 and i <= (LENT if u < last_unit else LAST_LENT):
+                lent.append("turn%d" % (i - 1))
+            if j + H_BANKS >= n_slots:
+                free_banks.append("h%d" % (j % H_BANKS))
+            budget = (FIRST_PIECES if u == 0 else PIECES_PER_SLOT)[i]
+            while finished:
+                drain(nc.scalar.copy)
+                budget = budget - 1
+            for n in range(budget):
+                if pieces:
+                    key, piece = take(pieces)
+                    interleave(nc.scalar.copy, key, piece, piece + 1)
+                    if piece == 3:
+                        to_quantize.append((max(j + 1, DUE[key]), key))
+
+        open_units.clear()
+        turn(last_unit, range(3))
+        turn(last_unit, range(3, 4))
+        quantize_feat(last_unit, 3)
+        run_passes(TAIL_FIRST)
+        for lo in (0, 64):
+            copy_turned(nc.scalar.copy, last_unit, 0, lo, lo + 64)
+            copy_turned(nc.vector.tensor_copy, last_unit, 1, lo, lo + 64)
+        for lo in (0, 64):
+            quantize_rows(last_unit, lo, lo + 64)
+        free_banks.extend(["turn0", "turn1"])
+        turn_of = 0
+        while moments or preds or running or finished:
+            while finished:
+                drain((nc.scalar.copy, nc.vector.tensor_copy)[turn_of % 2])
+                turn_of = turn_of + 1
+            run_passes(2)

@@ -22,24 +22,39 @@ HOLD = 3
 LENT = 0
 FEAT_QUANT_SLOT = 1
 GROUPS = (("zr", 0), ("zr", 1), ("zf", 0), ("zr", 2), ("zf", 1), ("zr", 3))
-DUE = {("w", 0, 1): 9, ("w", 1, 1): 17, ("y", 0, 0): 16, ("y", 1, 0): 19, ("w", 0, 2): 25, ("w", 1, 2): 33, ("w", 0, 3): 36, ("w", 1, 3): 41}
-V_Y = (11, 14)
-PRED_FROM = 40
-FIRST_PIECES = [2, 0, 1, 1, 1, 1, 1, 1]
-LAST_LENT = 0
-LATE_PASSES = [0, 0, 2, 2, 2, 2, 2, 1]
-LATE_FROM = 36
+DUE = {("w", 0, 1): 13, ("w", 1, 1): 14, ("y", 0, 0): 14, ("y", 1, 0): 21, ("w", 0, 2): 29, ("w", 1, 2): 30, ("w", 0, 3): 37, ("w", 1, 3): 39}
+FEAT_DUE = {0: 30, 1: 50, 2: 38, 3: 52, 4: 45, 6: 61}
+ROWS_DUE = {0: 13, 1: 21, 2: 29, 3: 35, 4: 54, 5: 60, 6: 58}
+POOL_HALVES = {0: 2, 1: 2, 2: 2, 4: 2, 6: 1}
+SCALAR_WEAVE = {3: (36, 38, 42, 44), 5: (48, 49, 50, 51), 6: (0, 0, 58, 59)}
+LEND = {58: ("turn0", "turn1")}
+CLOSE_TURN = (4, 5)
+CLOSE_ROWS_SLOT = 7
+LATE_ROWS_SLOT = 3
+LATE_WEAVE = (2, 3, 4, 5)
+WEAVE_LAG = 1
+AGE = 2
+SPLIT_FROM = 7
+ADD = mybir.AluOpType.add
+V_Y = ()
+PRED_FROM = 38
+FIRST_PIECES = [2, 0, 1, 1, 1, 1, 1, 2]
+LAST_LENT = 2
+LATE_PASSES = [1, 2, 2, 2, 2, 2, 2, 0]
+LAST_PASSES = [1, 2, 2, 2, 2, 2, 2, 2]
+LAST_FROM = 48
+LATE_FROM = 34
 RESULT_BUFS = 8
 H_BANKS = 3
 OUT_BANKS = 3
 PASSES_PER_SLOT = [0, 0, 1, 2, 1, 2, 1, 2]
-PIECES_PER_SLOT = [1, 0, 0, 1, 1, 2, 1, 2]
+PIECES_PER_SLOT = [0, 0, 1, 1, 2, 2, 1, 0]
 ROWS_QUANT_SLOT = 5
 X1_SLOT = 1
 LATE_FEAT = {1: 50, 3: 52}
 LEND_TURN = 99
 V_HEAD = 2
-TAIL_FIRST = 8
+TAIL = (4, 4)
 
 
 def take(queue):
@@ -173,8 +188,8 @@ def tile_random_maclaurin_features_s8_kernel(tc, x, w1, w2, c, r, v_words, v_sca
         def copy_x(g, half, src):
             dst = stage(("x", g, 0))
             nc.scalar.copy(
-                out=dst[:].bitcast(F32)[:, half * PASS : (half + 1) * PASS].rearrange("p (t m u) -> p t m u", t=2, u=2),
-                in_=src[:].rearrange("p (t u m) -> p t m u", t=2, u=2),
+                out=dst[:].bitcast(F32)[:, half * PASS : (half + 1) * PASS].rearrange("p (m e u) -> p m e u", e=2, u=2),
+                in_=src[:].rearrange("p (e u m) -> p m e u", e=2, u=2),
             )
 
         r_words = r_sb[:].bitcast(F32)
@@ -186,8 +201,8 @@ def tile_random_maclaurin_features_s8_kernel(tc, x, w1, w2, c, r, v_words, v_sca
                 q = 2 * g + h
                 nc.tensor.transpose(r_bank[:, quarter(h)], r_words[:, q : q + 1].to_broadcast([P, P]), ident[:])
             nc.scalar.copy(
-                out=r_all[:, g * PASS : (g + 1) * PASS].rearrange("p (h e m) -> p h e m", h=2, e=2),
-                in_=r_bank[:, 0 : 2 * P].bitcast(BF16).rearrange("p (h m e) -> p h e m", h=2, e=2),
+                out=r_all[:, g * PASS : (g + 1) * PASS],
+                in_=r_bank[:, 0 : 2 * P].bitcast(BF16),
             )
 
         spread_r(0)
@@ -220,75 +235,77 @@ def tile_random_maclaurin_features_s8_kernel(tc, x, w1, w2, c, r, v_words, v_sca
         fresh = []
         usable = set()
 
+        z_plain = {}
+
         def fill(j):
             u, i = divmod(j, 8)
             f, g = UNITS[u]
-            dst = bank("h%d" % (j % H_BANKS))
-            h_bank[j] = dst
-            if i < 4:
-                matmul(dst[:], operand(mx["w", 0, f], quarter(i)), operand(mx["x", g, 0], whole), True, True)
-            else:
-                for s in range(4):
-                    matmul(dst[:, quarter(s)], operand(mx["w", 1, f], quarter(s)), operand(mx["x", g, 0], quarter(i - 4)), True, True)
+            h_bank[j] = bank("h%d" % (j % H_BANKS))
+            matmul(h_bank[j][:], operand(mx["w", i // 4, f], quarter(i % 4)), operand(mx["x", g, 0], whole), True, True)
 
         def consume(j):
             u, i = divmod(j, 8)
             f, g = UNITS[u]
-            if i == 0:
-                scaled[u] = ring.tile([P, 4, PASS], F32, name="scaled", tag="scaled", bufs=2)
-                mx["zf", f, g] = mx_tiles("zf%d%d" % (f, g))
             if i < 4:
+                scaled[u, i] = ring.tile([P, PASS], F32, name="scaled", tag="scaled", bufs=5)
                 nc.vector.scalar_tensor_tensor(
-                    out=scaled[u][:, i, :], in0=h_bank[j][:], scalar=c_sb[:, 4 * f + i : 4 * f + i + 1],
+                    out=scaled[u, i][:], in0=h_bank[j][:], scalar=c_sb[:, 4 * f + i : 4 * f + i + 1],
                     in1=r_all[:, g * PASS : (g + 1) * PASS], op0=MULT, op1=MULT,
                 )
                 return
-            t = i - 4
-            if f == 3:
-                z_feat[u, t] = ring.tile([P, PASS], BF16, name="z_cell", tag="z_cell", bufs=8, align_bytes=64)
-            else:
-                if t == 0:
-                    z_feat[u, 4] = ring.tile([P, 4 * PASS], BF16, name="z_unit", tag="z_unit", bufs=4, align_bytes=64)
-                z_feat[u, t] = z_feat[u, 4][:, t * PASS : (t + 1) * PASS]
-            nc.vector.tensor_tensor(
-                out=z_feat[u, t][:].rearrange("p (n i s) -> p n s i", i=2, s=4),
-                in0=h_bank[j][:].rearrange("p (s n i) -> p n s i", s=4, i=2),
-                in1=scaled[u][:, :, quarter(t)].rearrange("p s (n i) -> p n s i", i=2),
-                op=MULT,
+            s = i - 4
+            if s == 0:
+                z_plain[u] = ring.tile([P, 4 * PASS], BF16, name="z_plain", tag="z_plain", bufs=3)
+            nc.vector.tensor_tensor(out=z_plain[u][:, s * PASS : (s + 1) * PASS], in0=h_bank[j][:], in1=scaled[u, s][:], op=MULT)
+
+        def weave_views(u):
+            if u not in z_feat:
+                z_feat[u] = ring.tile([P, 4 * PASS], BF16, name="z_feat", tag="z_feat", bufs=5, align_bytes=64)
+            return (
+                z_feat[u][:].rearrange("p (h e m s) -> p h e m s", h=2, e=2, s=4),
+                z_plain[u][:].rearrange("p (s h m e) -> p h e m s", s=4, h=2, e=2),
             )
 
-        def quantize_feat(u, t):
+        def weave_half(u, h):
+            dst, src = weave_views(u)
+            nc.gpsimd.tensor_scalar(out=dst[:, h], in0=src[:, h], scalar1=1.0, scalar2=0.0, op0=MULT, op1=ADD)
+
+        def weave_quarter(copy, u, t):
+            dst, src = weave_views(u)
+            copy(out=dst[:, t // 2, t % 2], in_=src[:, t // 2, t % 2])
+
+        def quantize_feat(u, lo, hi):
             f, g = UNITS[u]
-            quantize(mx["zf", f, g], quarter(t) if t < 4 else whole, z_feat[u, t][:])
+            if ("zf", f, g) not in mx:
+                mx["zf", f, g] = mx_tiles("zf%d%d" % (f, g))
+            quantize(mx["zf", f, g], slice(lo * P, hi * P), z_feat[u][:, lo * PASS : hi * PASS])
+            for t in range(lo, hi):
+                fresh.append((clock[0], ("zf", f, g, t)))
+
+        def turn(u, pair):
+            turned[u, pair] = bank("turn%d" % pair)
+            words = z_plain[u][:].bitcast(F32)
             for n in range(4):
-                if t in (n, 4):
-                    fresh.append(("zf", f, g, n))
+                nc.tensor.transpose(turned[u, pair][:, quarter(n)], words[:, quarter(4 * pair + n)], ident[:])
 
-        def turn(u, cells=range(4)):
-            for h in range(2):
-                if (u, h) not in turned:
-                    turned[u, h] = bank("turn%d" % h)
-                for t in cells:
-                    nc.tensor.transpose(turned[u, h][:, quarter(t)], z_feat[u, t][:].bitcast(F32)[:, h : 256 : 2], ident[:])
-
-        def copy_turned(copy, u, h, lo, hi):
-            if (u, 0) not in z_rows:
-                z_rows[u, 0] = ring.tile([P, 4 * PASS], BF16, name="z_rows", tag="z_rows", bufs=2, align_bytes=64)
+        def copy_turned(copy, u, pair):
+            if u not in z_rows:
+                z_rows[u] = ring.tile([P, 4 * PASS], BF16, name="z_rows", tag="z_rows", bufs=3, align_bytes=64)
             copy(
-                out=z_rows[u, 0][:].rearrange("m (p h e t) -> m h p e t", h=2, e=2, t=4)[:, h, lo:hi],
-                in_=turned[u, h][:].bitcast(BF16).rearrange("m (t p e) -> m p e t", t=4, e=2)[:, lo:hi],
+                out=z_rows[u][:].bitcast(F32)[:, pair * PASS : (pair + 1) * PASS].rearrange("m (s p h) -> m s p h", s=2, h=2),
+                in_=turned[u, pair][:].rearrange("m (s h p) -> m s p h", s=2, h=2),
             )
 
         def quantize_rows(u, lo, hi):
             f, g = UNITS[u]
             if ("zr", f, g) not in mx:
                 mx["zr", f, g] = mx_tiles("zr%d%d" % (f, g))
-            quantize(mx["zr", f, g], slice(4 * lo, 4 * hi), z_rows[u, 0][:, 16 * lo : 16 * hi])
-            for n in range(lo // 32, hi // 32):
-                fresh.append(("zr", f, g, n))
+            quantize(mx["zr", f, g], slice(lo * P, hi * P), z_rows[u][:, lo * PASS : hi * PASS])
+            for s in range(lo, hi):
+                fresh.append((clock[0], ("zr", f, g, s)))
 
         pred_rows = out_0.rearrange("(g m t) n -> g t m n", g=2, t=4)
-        moment_rows = out_1.rearrange("(f i m) n -> f i m n", f=4, i=4)
+        moment_rows = out_1.rearrange("(f m s) n -> f s m n", f=4, s=4)
         free_banks = ["out%d" % b for b in range(OUT_BANKS)]
         finished = []
         running = []
@@ -339,8 +356,8 @@ def tile_random_maclaurin_features_s8_kernel(tc, x, w1, w2, c, r, v_words, v_sca
                 running[:] = [other for other in running if other["tag"] != group["tag"]]
 
         def run_passes(count):
-            while fresh:
-                usable.add(take(fresh))
+            while fresh and (not open_units or fresh[0][0] <= clock[0] - AGE):
+                usable.add(take(fresh)[1])
             for step in range(count):
                 one_pass()
 
@@ -362,42 +379,50 @@ def tile_random_maclaurin_features_s8_kernel(tc, x, w1, w2, c, r, v_words, v_sca
             clock[0] = j
             if i == 0 and u > 0:
                 assert not lent and all(group["tag"][0] != "t" for group in running)
-                turn(u - 1)
+                for pair in range(1 if u - 1 >= SPLIT_FROM else 0, 2):
+                    turn(u - 1, pair)
+            if i == 6 and u >= SPLIT_FROM:
+                assert "turn0" not in lent and all(group["tag"] != "turn0" for group in running)
+                turn(u, 0)
             if j + ahead < n_slots:
                 fill(j + ahead)
             if j == X1_SLOT:
                 x_banks = [transpose_x(1, half, "turn%d" % half) for half in range(2)]
+            lent.extend(LEND.get(j, ()))
             if j >= 10:
-                run_passes((LATE_PASSES if j >= LATE_FROM else PASSES_PER_SLOT)[i])
+                run_passes((LAST_PASSES if j >= LAST_FROM else LATE_PASSES if j >= LATE_FROM else PASSES_PER_SLOT)[i])
+            closing = u > 0 and UNITS[u - 1][0] == 3
+            turn_at = CLOSE_TURN if closing else (0, 1)
+            if i == 0:
+                for h in range(POOL_HALVES.get(u - 1, 0)):
+                    weave_half(u - 1, h)
             consume(j)
+            for early in ROWS_DUE:
+                if ROWS_DUE[early] == j:
+                    quantize_rows(early, 0, 4)
+            if i == 7 and u >= SPLIT_FROM:
+                quantize_rows(u, 0, 2)
             for due, key in to_quantize:
                 if due == j:
                     quantize_staged(key)
-            if j in V_Y:
-                half = V_Y.index(j)
-                interleave(nc.vector.tensor_copy, ("y", 0, 0), 2 * half, 2 * half + 2)
-                if half == 1:
-                    to_quantize.append((DUE["y", 0, 0], ("y", 0, 0)))
-            if i == FEAT_QUANT_SLOT and u > 0 and UNITS[u - 1][0] < 3 and u - 1 not in LATE_FEAT:
-                quantize_feat(u - 1, 4)
-            for late in LATE_FEAT:
-                if LATE_FEAT[late] == j + 1:
-                    quantize_feat(late, 4)
-            if i == 0 and u > 0 and UNITS[u - 1][0] == 3:
-                quantize_feat(u - 1, 3)
-            if f == 3 and i > 4:
-                quantize_feat(u, i - 5)
-            if i == ROWS_QUANT_SLOT and u > 0:
-                quantize_rows(u - 1, 0, P)
+            if closing and j - WEAVE_LAG in SCALAR_WEAVE[u - 1]:
+                t = SCALAR_WEAVE[u - 1].index(j - WEAVE_LAG)
+                quantize_feat(u - 1, t, t + 1)
+            for early in FEAT_DUE:
+                if FEAT_DUE[early] == j:
+                    quantize_feat(early, 0, 4)
             if j == X1_SLOT:
                 for half in range(2):
                     copy_x(1, half, x_banks[half])
-            if i in (1, 2) and u > 0:
-                copy_turned(nc.scalar.copy, u - 1, i - 1, 0, P)
-            if i in (1, 2) and u > 0 and UNITS[u - 1][1] == 1 and i <= (LENT if u < last_unit else LAST_LENT):
-                lent.append("turn%d" % (i - 1))
+            if u > 0 and i in turn_at:
+                copy_turned(nc.scalar.copy, u - 1, turn_at.index(i))
+            if i == 6 and u >= SPLIT_FROM:
+                copy_turned(nc.scalar.copy, u, 0)
             if j + H_BANKS >= n_slots:
                 free_banks.append("h%d" % (j % H_BANKS))
+            for early in SCALAR_WEAVE:
+                if j and j in SCALAR_WEAVE[early]:
+                    weave_quarter(nc.scalar.copy, early, SCALAR_WEAVE[early].index(j))
             budget = (FIRST_PIECES if u == 0 else PIECES_PER_SLOT)[i]
             while finished:
                 drain(nc.scalar.copy)
@@ -407,22 +432,34 @@ def tile_random_maclaurin_features_s8_kernel(tc, x, w1, w2, c, r, v_words, v_sca
                     key, piece = take(pieces)
                     interleave(nc.scalar.copy, key, piece, piece + 1)
                     if piece == 3:
-                        to_quantize.append((max(j + 1, DUE[key]), key))
+                        assert DUE[key] > j
+                        to_quantize.append((DUE[key], key))
 
         open_units.clear()
-        turn(last_unit, range(3))
-        turn(last_unit, range(3, 4))
-        quantize_feat(last_unit, 3)
-        run_passes(TAIL_FIRST)
-        for lo in (0, 64):
-            copy_turned(nc.scalar.copy, last_unit, 0, lo, lo + 64)
-            copy_turned(nc.vector.tensor_copy, last_unit, 1, lo, lo + 64)
-        for lo in (0, 64):
-            quantize_rows(last_unit, lo, lo + 64)
-        free_banks.extend(["turn0", "turn1"])
+        clock[0] = 2 * n_slots
+        free_banks.append("turn0")
+        assert not lent and all(group["tag"] != "turn1" for group in running)
+        turn(last_unit, 1)
+        copy_turned(nc.scalar.copy, last_unit, 1)
+        free_banks.append("turn1")
+        run_passes(TAIL[0])
+        weave_quarter(nc.vector.tensor_copy, last_unit, 0)
+        weave_quarter(nc.vector.tensor_copy, last_unit, 1)
+        quantize_feat(last_unit, 0, 1)
+        weave_quarter(nc.vector.tensor_copy, last_unit, 2)
+        quantize_feat(last_unit, 1, 2)
+        while finished:
+            drain(nc.scalar.copy)
+        run_passes(TAIL[1])
+        weave_quarter(nc.vector.tensor_copy, last_unit, 3)
+        quantize_feat(last_unit, 2, 3)
+        quantize_rows(last_unit, 2, 4)
+        quantize_feat(last_unit, 3, 4)
+        while finished:
+            drain(nc.scalar.copy)
         turn_of = 0
         while moments or preds or running or finished:
-            while finished:
-                drain((nc.scalar.copy, nc.vector.tensor_copy)[turn_of % 2])
-                turn_of = turn_of + 1
             run_passes(2)
+            while finished:
+                drain((nc.vector.tensor_copy, nc.scalar.copy)[turn_of % 2])
+                turn_of = turn_of + 1

@@ -22,11 +22,11 @@ HOLD = 3
 LENT = 0
 FEAT_QUANT_SLOT = 1
 GROUPS = (("zr", 0), ("zr", 1), ("zf", 0), ("zr", 2), ("zf", 1), ("zr", 3))
-DUE = {("w", 0, 1): 13, ("w", 1, 1): 14, ("y", 0, 0): 14, ("y", 1, 0): 21, ("w", 0, 2): 29, ("w", 1, 2): 30, ("w", 0, 3): 37, ("w", 1, 3): 39}
-FEAT_DUE = {0: 30, 1: 50, 2: 38, 3: 52, 4: 45, 6: 61}
-ROWS_DUE = {0: 13, 1: 21, 2: 29, 3: 35, 4: 54, 5: 60, 6: 58}
+DUE = {("w", 0, 1): 14, ("w", 1, 1): 14, ("y", 0, 0): 22, ("y", 1, 0): 22, ("w", 0, 2): 30, ("w", 1, 2): 30, ("w", 0, 3): 36, ("w", 1, 3): 39}
+FEAT_DUE = {0: 33, 1: 50, 2: 38, 3: 52, 4: 46, 6: 61}
+ROWS_DUE = {0: 14, 1: 22, 2: 30, 3: 35, 4: 54, 5: 60, 6: 58}
 POOL_HALVES = {0: 2, 1: 2, 2: 2, 4: 2, 6: 1}
-SCALAR_WEAVE = {3: (36, 38, 42, 44), 5: (48, 49, 50, 51), 6: (0, 0, 58, 59)}
+SCALAR_WEAVE = {3: (36, 38, 42, 44), 5: (48, 48, 49, 49), 6: (0, 0, 58, 59)}
 LEND = {58: ("turn0", "turn1")}
 CLOSE_TURN = (4, 5)
 CLOSE_ROWS_SLOT = 7
@@ -34,6 +34,10 @@ LATE_ROWS_SLOT = 3
 LATE_WEAVE = (2, 3, 4, 5)
 WEAVE_LAG = 1
 AGE = 2
+R1_SLOT = 3
+HALVED = 1
+CLOSE_DUE = (50, 51)
+LAST_SPLIT = 1
 SPLIT_FROM = 7
 ADD = mybir.AluOpType.add
 V_Y = ()
@@ -45,12 +49,15 @@ LAST_PASSES = [1, 2, 2, 2, 2, 2, 2, 2]
 LAST_FROM = 48
 LATE_FROM = 34
 RESULT_BUFS = 8
-H_BANKS = 3
-OUT_BANKS = 3
+H_BANKS = 4
+OUT_BANKS = 2
+PAIRED_UNTIL = 36
+SPLIT_UNITS = (0, 1, 2, 3, 7)
 PASSES_PER_SLOT = [0, 0, 1, 2, 1, 2, 1, 2]
 PIECES_PER_SLOT = [0, 0, 1, 1, 2, 2, 1, 0]
 ROWS_QUANT_SLOT = 5
 X1_SLOT = 1
+X1_DUE = 4
 LATE_FEAT = {1: 50, 3: 52}
 LEND_TURN = 99
 V_HEAD = 2
@@ -206,7 +213,6 @@ def tile_random_maclaurin_features_s8_kernel(tc, x, w1, w2, c, r, v_words, v_sca
             )
 
         spread_r(0)
-        spread_r(1)
         x_banks = [transpose_x(0, half, "turn%d" % half) for half in range(2)]
         for half in range(2):
             copy_x(0, half, x_banks[half])
@@ -225,7 +231,7 @@ def tile_random_maclaurin_features_s8_kernel(tc, x, w1, w2, c, r, v_words, v_sca
 
         prep = [("w", 0, 1), ("w", 1, 1), ("y", 0, 0), ("y", 1, 0), ("w", 0, 2), ("w", 1, 2), ("w", 0, 3), ("w", 1, 3)]
         pieces = [(key, i) for key in prep for i in range(4) if key != ("y", 0, 0) or not V_Y]
-        to_quantize = [(1, ("w", 1, 0)), (X1_SLOT + 3, ("x", 1, 0))]
+        to_quantize = [(1, ("w", 1, 0)), (X1_DUE, ("x", 1, 0))]
 
         h_bank = {}
         scaled = {}
@@ -236,12 +242,16 @@ def tile_random_maclaurin_features_s8_kernel(tc, x, w1, w2, c, r, v_words, v_sca
         usable = set()
 
         z_plain = {}
+        h_tag = {}
+        h_free = ["h%d" % b for b in range(H_BANKS)]
 
         def fill(j):
             u, i = divmod(j, 8)
             f, g = UNITS[u]
-            h_bank[j] = bank("h%d" % (j % H_BANKS))
-            matmul(h_bank[j][:], operand(mx["w", i // 4, f], quarter(i % 4)), operand(mx["x", g, 0], whole), True, True)
+            h_tag[j] = take(h_free)
+            h_bank[j] = bank(h_tag[j])
+            for cols in (slice(0, 256), slice(256, 512)) if j < HALVED else (whole,):
+                matmul(h_bank[j][:, cols], operand(mx["w", i // 4, f], quarter(i % 4)), operand(mx["x", g, 0], cols), True, True)
 
         def consume(j):
             u, i = divmod(j, 8)
@@ -370,22 +380,28 @@ def tile_random_maclaurin_features_s8_kernel(tc, x, w1, w2, c, r, v_words, v_sca
                 free_banks.append(tag)
 
         open_units = [1]
-        ahead = H_BANKS - 1
-        for j in range(ahead):
+        for j in range(2):
             fill(j)
         for j in range(n_slots):
             u, i = divmod(j, 8)
             f, g = UNITS[u]
             clock[0] = j
-            if i == 0 and u > 0:
+            if j > PAIRED_UNTIL:
+                targets = (j + 1, j + 2)
+            else:
+                targets = (j + 2, j + 1, j + 4) if j % 2 else (j + 3, j + 2)
+            if i == 0 and u > 0 and u - 1 not in SPLIT_UNITS:
                 assert not lent and all(group["tag"][0] != "t" for group in running)
-                for pair in range(1 if u - 1 >= SPLIT_FROM else 0, 2):
-                    turn(u - 1, pair)
-            if i == 6 and u >= SPLIT_FROM:
+                turn(u - 1, 0)
+                turn(u - 1, 1)
+            for target in targets:
+                if target < n_slots and target not in h_bank and ("w", target % 8 // 4, UNITS[target // 8][0]) in mx and ("x", UNITS[target // 8][1], 0) in mx:
+                    fill(target)
+            if i == 0 and u - 1 in SPLIT_UNITS:
+                turn(u - 1, 1)
+            if i == 6 and u in SPLIT_UNITS:
                 assert "turn0" not in lent and all(group["tag"] != "turn0" for group in running)
                 turn(u, 0)
-            if j + ahead < n_slots:
-                fill(j + ahead)
             if j == X1_SLOT:
                 x_banks = [transpose_x(1, half, "turn%d" % half) for half in range(2)]
             lent.extend(LEND.get(j, ()))
@@ -397,32 +413,40 @@ def tile_random_maclaurin_features_s8_kernel(tc, x, w1, w2, c, r, v_words, v_sca
                 for h in range(POOL_HALVES.get(u - 1, 0)):
                     weave_half(u - 1, h)
             consume(j)
-            for early in ROWS_DUE:
-                if ROWS_DUE[early] == j:
-                    quantize_rows(early, 0, 4)
-            if i == 7 and u >= SPLIT_FROM:
-                quantize_rows(u, 0, 2)
+            if j == PAIRED_UNTIL or len(h_bank) + len(h_free) >= n_slots:
+                free_banks.append(h_tag[j])
+            else:
+                h_free.append(h_tag[j])
             for due, key in to_quantize:
                 if due == j:
                     quantize_staged(key)
-            if closing and j - WEAVE_LAG in SCALAR_WEAVE[u - 1]:
-                t = SCALAR_WEAVE[u - 1].index(j - WEAVE_LAG)
-                quantize_feat(u - 1, t, t + 1)
+            for early in ROWS_DUE:
+                if ROWS_DUE[early] == j:
+                    quantize_rows(early, 0, 4)
+            if i == 7 and u == last_unit:
+                quantize_rows(u, 0, 2)
+            if j in CLOSE_DUE:
+                step = 4 // len(CLOSE_DUE)
+                n = CLOSE_DUE.index(j)
+                quantize_feat(u - 1, n * step, (n + 1) * step)
             for early in FEAT_DUE:
                 if FEAT_DUE[early] == j:
                     quantize_feat(early, 0, 4)
             if j == X1_SLOT:
                 for half in range(2):
                     copy_x(1, half, x_banks[half])
-            if u > 0 and i in turn_at:
+            if j == R1_SLOT:
+                spread_r(1)
+            if i == 0 and u - 1 in SPLIT_UNITS:
+                copy_turned(nc.scalar.copy, u - 1, 1)
+            if u > 0 and i in turn_at and u - 1 not in SPLIT_UNITS:
                 copy_turned(nc.scalar.copy, u - 1, turn_at.index(i))
-            if i == 6 and u >= SPLIT_FROM:
+            if i == 6 and u in SPLIT_UNITS:
                 copy_turned(nc.scalar.copy, u, 0)
-            if j + H_BANKS >= n_slots:
-                free_banks.append("h%d" % (j % H_BANKS))
             for early in SCALAR_WEAVE:
-                if j and j in SCALAR_WEAVE[early]:
-                    weave_quarter(nc.scalar.copy, early, SCALAR_WEAVE[early].index(j))
+                for t, due in enumerate(SCALAR_WEAVE[early]):
+                    if j and due == j:
+                        weave_quarter(nc.scalar.copy, early, t)
             budget = (FIRST_PIECES if u == 0 else PIECES_PER_SLOT)[i]
             while finished:
                 drain(nc.scalar.copy)

@@ -14,54 +14,23 @@ U8 = mybir.dt.uint8
 FP8X4 = mybir.dt.float8_e4m3fn_x4
 FP4X4 = mybir.dt.float4_e2m1fn_x4
 MULT = mybir.AluOpType.mult
+ADD = mybir.AluOpType.add
 
 P = 128
 PASS = 512
+STEPS = 8
+
 UNITS = [(0, 0), (0, 1), (1, 0), (1, 1), (2, 0), (3, 0), (2, 1), (3, 1)]
-HOLD = 3
-LENT = 0
-FEAT_QUANT_SLOT = 1
-GROUPS = (("zr", 0), ("zr", 1), ("zf", 0), ("zr", 2), ("zf", 1), ("zr", 3))
-DUE = {("w", 0, 1): 14, ("w", 1, 1): 14, ("y", 0, 0): 22, ("y", 1, 0): 22, ("w", 0, 2): 30, ("w", 1, 2): 30, ("w", 0, 3): 36, ("w", 1, 3): 39}
-FEAT_DUE = {0: 33, 1: 50, 2: 38, 3: 52, 4: 46, 6: 61}
-ROWS_DUE = {0: 14, 1: 22, 2: 30, 3: 35, 4: 54, 5: 60, 6: 58}
+HALF = len(UNITS) // 2
+LAST = len(UNITS) - 1
+
+LAG = 2
+QUIET = 6
 POOL_HALVES = {0: 2, 1: 2, 2: 2, 4: 2, 6: 1}
-SCALAR_WEAVE = {3: (36, 38, 42, 44), 5: (48, 48, 49, 49), 6: (0, 0, 58, 59)}
-LEND = {58: ("turn0", "turn1")}
-CLOSE_TURN = (4, 5)
-CLOSE_ROWS_SLOT = 7
-LATE_ROWS_SLOT = 3
-LATE_WEAVE = (2, 3, 4, 5)
-WEAVE_LAG = 1
-AGE = 2
-R1_SLOT = 3
-HALVED = 1
-CLOSE_DUE = (50, 51)
-LAST_SPLIT = 1
-SPLIT_FROM = 7
-ADD = mybir.AluOpType.add
-V_Y = ()
-PRED_FROM = 38
-FIRST_PIECES = [2, 0, 1, 1, 1, 1, 1, 2]
-LAST_LENT = 2
-LATE_PASSES = [1, 2, 2, 2, 2, 2, 2, 0]
-LAST_PASSES = [1, 2, 2, 2, 2, 2, 2, 2]
-LAST_FROM = 48
-LATE_FROM = 34
-RESULT_BUFS = 8
-H_BANKS = 4
-OUT_BANKS = 2
-PAIRED_UNTIL = 36
-SPLIT_UNITS = (0, 1, 2, 3, 7)
-PASSES_PER_SLOT = [0, 0, 1, 2, 1, 2, 1, 2]
-PIECES_PER_SLOT = [0, 0, 1, 1, 2, 2, 1, 0]
-ROWS_QUANT_SLOT = 5
-X1_SLOT = 1
-X1_DUE = 4
-LATE_FEAT = {1: 50, 3: 52}
-LEND_TURN = 99
-V_HEAD = 2
-TAIL = (4, 4)
+ROWS_SOON = {3: 3, 6: 2}
+PARKED = (1, QUIET)
+POOL_Y = 2
+ENDING_PASSES = 4
 
 
 def take(queue):
@@ -70,10 +39,19 @@ def take(queue):
     return first
 
 
+def quarter(i):
+    return slice(i * P, (i + 1) * P)
+
+
+def first_unit_with(f):
+    return min(u for u in range(len(UNITS)) if UNITS[u][0] == f)
+
+
 def tile_random_maclaurin_features_s8_kernel(tc, x, w1, w2, c, r, v_words, v_scales, y, out_0, out_1):
     nc = tc.nc
-    n_slots = 8 * len(UNITS)
-    last_unit = len(UNITS) - 1
+    n_steps = STEPS * len(UNITS)
+    whole = slice(0, PASS)
+    halves = (slice(0, PASS // 2), slice(PASS // 2, PASS))
 
     with ExitStack() as ctx:
         keep = ctx.enter_context(tc.tile_pool(name="keep", bufs=1))
@@ -89,19 +67,17 @@ def tile_random_maclaurin_features_s8_kernel(tc, x, w1, w2, c, r, v_words, v_sca
             scales = keep.tile([P, PASS], U8, name=name + "_scales", align_bytes=64)
             return codes, scales
 
-        def quantize(mx, cols, src):
-            nc.vector.quantize_mx(out=mx[0][:, cols].bitcast(FP8X4), scales=mx[1][:, cols], in_=src)
+        def quantize(tiles, cols, src):
+            nc.vector.quantize_mx(out=tiles[0][:, cols].bitcast(FP8X4), scales=tiles[1][:, cols], in_=src)
 
-        def operand(mx, cols):
-            return mx[0][:, cols].bitcast(FP8X4), mx[1][:, cols]
+        def operand(tiles, cols):
+            return tiles[0][:, cols].bitcast(FP8X4), tiles[1][:, cols]
 
         def matmul(out, lhs, rhs, start, stop):
             nc.tensor.matmul_mx(out=out, lhsT=lhs[0], lhsT_scale=lhs[1], rhs=rhs[0], rhs_scale=rhs[1], start=start, stop=stop)
 
-        whole = slice(0, PASS)
-
-        def quarter(i):
-            return slice(i * P, (i + 1) * P)
+        def pool_copy(out, in_):
+            nc.gpsimd.tensor_scalar(out=out, in0=in_, scalar1=1.0, scalar2=0.0, op0=MULT, op1=ADD)
 
         r_sb = keep.tile([P, 8], BF16, name="r_sb")
         nc.scalar.dma_start(out=r_sb[:].rearrange("m (g t) -> m g t", g=2), in_=r.rearrange("(g m t) -> m g t", g=2, t=4))
@@ -110,44 +86,37 @@ def tile_random_maclaurin_features_s8_kernel(tc, x, w1, w2, c, r, v_words, v_sca
 
         ident = keep.tile([P, P], F32, name="ident")
         make_identity(nc, ident[:])
-        v_plane = keep.tile([P, 4 * C], U8, name="v_plane", align_bytes=64)
-        nc.gpsimd.memset(v_plane[:].bitcast(I32), 0)
+        v_scale_sb = keep.tile([P, 4 * C], U8, name="v_scale_sb", align_bytes=64)
+        nc.gpsimd.memset(v_scale_sb[:].bitcast(I32), 0)
 
-        raw = {}
+        loaded = {}
         x_rows = x.rearrange("(g m t) k -> g m (t k)", g=2, t=4)
+        w_rows = [w.rearrange("(p j) d -> p j d", j=4) for w in (w1, w2)]
+        y_rows = y.rearrange("(g p j) n -> g p j n", g=2, j=4)
 
         def load_x(g):
-            for half in range(2):
-                tile = keep.tile([P, 2 * K], BF16, name="x_raw%d%d" % (g, half))
-                nc.sync.dma_start(out=tile[:], in_=x_rows[g][:, half * 2 * K : (half + 1) * 2 * K])
-                raw["x", g, half] = tile
+            for h in range(2):
+                tile = keep.tile([P, 2 * K], BF16, name="x_in%d%d" % (g, h))
+                nc.sync.dma_start(out=tile[:], in_=x_rows[g][:, h * 2 * K : (h + 1) * 2 * K])
+                loaded["x", g, h] = tile
 
-        def load_w(which, f):
-            tile = keep.tile([P, 4, PASS], BF16, name="w_raw%d%d" % (which, f))
-            src = (w1, w2)[which].rearrange("(p j) d -> p j d", j=4)
-            nc.sync.dma_start(out=tile[:], in_=src[:, :, f * PASS : (f + 1) * PASS])
-            raw["w", which, f] = tile
+        def load_k_first(key, src):
+            tile = keep.tile([P, 4, src.shape[2]], BF16, name="%s_in%d%d" % key)
+            nc.sync.dma_start(out=tile[:], in_=src)
+            loaded[key] = tile
 
-        def load_w_half(half):
-            tile = keep.tile([P, 4, PASS // 2], BF16, name="w_first%d" % half)
-            src = w1.rearrange("(p j) d -> p j d", j=4)
-            nc.sync.dma_start(out=tile[:], in_=src[:, :, half * 256 : (half + 1) * 256])
-            raw["half", half] = tile
-
-        def load_y(g):
-            tile = keep.tile([P, 4, R], BF16, name="y_raw%d" % g)
-            nc.sync.dma_start(out=tile[:], in_=y.rearrange("(g p j) n -> g p j n", g=2, j=4)[g])
-            raw["y", g, 0] = tile
+        def load_w(n, f):
+            load_k_first(("w", n, f), w_rows[n][:, :, f * PASS : (f + 1) * PASS])
 
         load_x(0)
-        load_w_half(0)
-        load_w_half(1)
+        for n in range(2):
+            load_k_first(("w_first", n, 0), w_rows[0][:, :, halves[n]])
         load_w(1, 0)
         load_x(1)
         load_w(0, 1)
+        load_k_first(("y", 0, 0), y_rows[0])
         load_w(1, 1)
-        load_y(0)
-        load_y(1)
+        load_k_first(("y", 1, 0), y_rows[1])
         for f in (2, 3):
             load_w(0, f)
             load_w(1, f)
@@ -155,7 +124,7 @@ def tile_random_maclaurin_features_s8_kernel(tc, x, w1, w2, c, r, v_words, v_sca
         nc.sync.dma_start(out=v_codes[:].bitcast(I32), in_=v_words.bitcast(I32).rearrange("f p n -> p f n"))
         for q in range(4):
             nc.sync.dma_start(
-                out=v_plane[:].bitcast(I32)[32 * q : 32 * q + 4, :].rearrange("p (f n) -> p f n", f=4),
+                out=v_scale_sb[:].bitcast(I32)[32 * q : 32 * q + 4, :].rearrange("p (f n) -> p f n", f=4),
                 in_=v_scales.bitcast(I32)[:, 4 * q : 4 * q + 4, :].rearrange("f p n -> p f n"),
             )
 
@@ -164,38 +133,40 @@ def tile_random_maclaurin_features_s8_kernel(tc, x, w1, w2, c, r, v_words, v_sca
 
         def stage(key):
             if key not in staged:
-                staged[key] = ring.tile([P, 4 * PASS], BF16, name="stage", tag="stage", bufs=5, align_bytes=64)
+                staged[key] = ring.tile([P, 4 * PASS], BF16, name="stage", tag="stage", bufs=6, align_bytes=64)
             return staged[key]
 
+        def weight_views(key, src):
+            return (
+                stage(key)[:].rearrange("p (s a b j) -> p a s b j", s=4, b=2, j=4),
+                src[:].rearrange("p j (a b s) -> p a s b j", b=2, s=4),
+            )
+
         def interleave(copy, key, lo, hi):
-            dst = stage(key)
             if key[0] == "w":
-                copy(
-                    out=dst[:].rearrange("p (s a b j) -> p a s b j", s=4, b=2, j=4)[:, 16 * lo : 16 * hi],
-                    in_=raw[key][:].rearrange("p j (a b s) -> p a s b j", b=2, s=4)[:, 16 * lo : 16 * hi],
-                )
+                dst, src = weight_views(key, loaded[key])
+                copy(out=dst[:, 16 * lo : 16 * hi], in_=src[:, 16 * lo : 16 * hi])
             else:
                 copy(
-                    out=dst[:].rearrange("p (a i j) -> p a j i", i=4, j=4)[:, 32 * lo : 32 * hi],
-                    in_=raw[key][:].rearrange("p j (a i) -> p a j i", i=4)[:, 32 * lo : 32 * hi],
+                    out=stage(key)[:].rearrange("p (a i j) -> p a j i", i=4, j=4)[:, 32 * lo : 32 * hi],
+                    in_=loaded[key][:].rearrange("p j (a i) -> p a j i", i=4)[:, 32 * lo : 32 * hi],
                 )
 
         def quantize_staged(key):
             mx[key] = mx_tiles("%s%d%d" % key)
             quantize(mx[key], whole, staged[key][:])
 
-        def transpose_x(g, half, tag):
-            dst = bank(tag)
-            words = raw["x", g, half][:].bitcast(F32)
-            for t in range(2):
+        def turn_x(g, h):
+            dst = bank("turn%d" % h)
+            words = loaded["x", g, h][:].bitcast(F32)
+            for e in range(2):
                 for u in range(2):
-                    nc.tensor.transpose(dst[:, quarter(2 * t + u)], words[:, 256 * t + u : 256 * (t + 1) : 2], ident[:])
+                    nc.tensor.transpose(dst[:, quarter(2 * e + u)], words[:, 256 * e + u : 256 * (e + 1) : 2], ident[:])
             return dst
 
-        def copy_x(g, half, src):
-            dst = stage(("x", g, 0))
+        def copy_x(g, h, src):
             nc.scalar.copy(
-                out=dst[:].bitcast(F32)[:, half * PASS : (half + 1) * PASS].rearrange("p (m e u) -> p m e u", e=2, u=2),
+                out=stage(("x", g, 0))[:].bitcast(F32)[:, h * PASS : (h + 1) * PASS].rearrange("p (m e u) -> p m e u", e=2, u=2),
                 in_=src[:].rearrange("p (e u m) -> p m e u", e=2, u=2),
             )
 
@@ -205,68 +176,73 @@ def tile_random_maclaurin_features_s8_kernel(tc, x, w1, w2, c, r, v_words, v_sca
         def spread_r(g):
             r_bank = bank("out%d" % g)
             for h in range(2):
-                q = 2 * g + h
-                nc.tensor.transpose(r_bank[:, quarter(h)], r_words[:, q : q + 1].to_broadcast([P, P]), ident[:])
-            nc.scalar.copy(
-                out=r_all[:, g * PASS : (g + 1) * PASS],
-                in_=r_bank[:, 0 : 2 * P].bitcast(BF16),
-            )
+                word = r_words[:, 2 * g + h : 2 * g + h + 1]
+                nc.tensor.transpose(r_bank[:, quarter(h)], word.to_broadcast([P, P]), ident[:])
+            nc.scalar.copy(out=r_all[:, g * PASS : (g + 1) * PASS], in_=r_bank[:, 0 : 2 * P].bitcast(BF16))
 
         spread_r(0)
-        x_banks = [transpose_x(0, half, "turn%d" % half) for half in range(2)]
-        for half in range(2):
-            copy_x(0, half, x_banks[half])
-        for half in range(2):
-            nc.vector.tensor_copy(
-                out=stage(("w", 0, 0))[:].rearrange("p (s a b j) -> p a s b j", s=4, b=2, j=4)[:, 32 * half : 32 * half + 32],
-                in_=raw["half", half][:].rearrange("p j (a b s) -> p a s b j", b=2, s=4),
-            )
+        x_banks = [turn_x(0, h) for h in range(2)]
+        for h in range(2):
+            copy_x(0, h, x_banks[h])
+        for n in range(2):
+            dst, src = weight_views(("w", 0, 0), loaded["w_first", n, 0])
+            nc.vector.tensor_copy(out=dst[:, 32 * n : 32 * n + 32], in_=src)
         mx["x", 0, 0] = mx_tiles("x00")
-        quantize(mx["x", 0, 0], slice(0, 256), staged["x", 0, 0][:, 0:1024])
+        quantize(mx["x", 0, 0], halves[0], staged["x", 0, 0][:, 0 : 2 * PASS])
         quantize_staged(("w", 0, 0))
-        quantize(mx["x", 0, 0], slice(256, 512), staged["x", 0, 0][:, 1024:2048])
-        if V_HEAD:
-            interleave(nc.vector.tensor_copy, ("w", 1, 0), 0, V_HEAD)
-        interleave(nc.scalar.copy, ("w", 1, 0), V_HEAD, 4)
+        quantize(mx["x", 0, 0], halves[1], staged["x", 0, 0][:, 2 * PASS : 4 * PASS])
+        interleave(nc.vector.tensor_copy, ("w", 1, 0), 0, 2)
+        interleave(nc.scalar.copy, ("w", 1, 0), 2, 4)
 
-        prep = [("w", 0, 1), ("w", 1, 1), ("y", 0, 0), ("y", 1, 0), ("w", 0, 2), ("w", 1, 2), ("w", 0, 3), ("w", 1, 3)]
-        pieces = [(key, i) for key in prep for i in range(4) if key != ("y", 0, 0) or not V_Y]
-        to_quantize = [(1, ("w", 1, 0)), (X1_DUE, ("x", 1, 0))]
+        x_step = 1
+        input_due = {("w", 1, 0): 1, ("x", 1, 0): x_step + 1 + LAG}
+        for f in (1, 2):
+            for n in range(2):
+                input_due["w", n, f] = STEPS * (first_unit_with(f) - 1) + QUIET
+            if f == 1:
+                for g in range(2):
+                    input_due["y", g, 0] = STEPS * 2 + QUIET
+        input_due["w", 0, 3] = STEPS * first_unit_with(3) - 2 - LAG
+        input_due["w", 1, 3] = STEPS * first_unit_with(3) - 1
+        later_inputs = [key for key in input_due if key[0] == "y" or key[2] > 0]
+        scalar_quarters = [(key, i) for key in later_inputs for i in range(POOL_Y if key == ("y", 0, 0) else 0, 4)]
 
+        h_free = ["h%d" % b for b in range(4)]
+        h_tag = {}
         h_bank = {}
         scaled = {}
+        z_plain = {}
         z_feat = {}
         z_rows = {}
         turned = {}
         fresh = []
         usable = set()
 
-        z_plain = {}
-        h_tag = {}
-        h_free = ["h%d" % b for b in range(H_BANKS)]
+        def h_operands(j):
+            f, g = UNITS[j // STEPS]
+            return ("w", j % STEPS // 4, f), ("x", g, 0)
 
         def fill(j):
-            u, i = divmod(j, 8)
-            f, g = UNITS[u]
+            weight, rows = h_operands(j)
             h_tag[j] = take(h_free)
             h_bank[j] = bank(h_tag[j])
-            for cols in (slice(0, 256), slice(256, 512)) if j < HALVED else (whole,):
-                matmul(h_bank[j][:, cols], operand(mx["w", i // 4, f], quarter(i % 4)), operand(mx["x", g, 0], cols), True, True)
+            for cols in halves if j == 0 else (whole,):
+                matmul(h_bank[j][:, cols], operand(mx[weight], quarter(j % 4)), operand(mx[rows], cols), True, True)
 
-        def consume(j):
-            u, i = divmod(j, 8)
+        def multiply(j):
+            u, i = divmod(j, STEPS)
             f, g = UNITS[u]
+            s = i % 4
             if i < 4:
-                scaled[u, i] = ring.tile([P, PASS], F32, name="scaled", tag="scaled", bufs=5)
+                scaled[s] = ring.tile([P, PASS], F32, name="scaled", tag="scaled", bufs=5)
                 nc.vector.scalar_tensor_tensor(
-                    out=scaled[u, i][:], in0=h_bank[j][:], scalar=c_sb[:, 4 * f + i : 4 * f + i + 1],
+                    out=scaled[s][:], in0=h_bank[j][:], scalar=c_sb[:, 4 * f + s : 4 * f + s + 1],
                     in1=r_all[:, g * PASS : (g + 1) * PASS], op0=MULT, op1=MULT,
                 )
-                return
-            s = i - 4
-            if s == 0:
-                z_plain[u] = ring.tile([P, 4 * PASS], BF16, name="z_plain", tag="z_plain", bufs=3)
-            nc.vector.tensor_tensor(out=z_plain[u][:, s * PASS : (s + 1) * PASS], in0=h_bank[j][:], in1=scaled[u, s][:], op=MULT)
+            else:
+                if s == 0:
+                    z_plain[u] = ring.tile([P, 4 * PASS], BF16, name="z_plain", tag="z_plain", bufs=3)
+                nc.vector.tensor_tensor(out=z_plain[u][:, s * PASS : (s + 1) * PASS], in0=h_bank[j][:], in1=scaled[s][:], op=MULT)
 
         def weave_views(u):
             if u not in z_feat:
@@ -278,19 +254,11 @@ def tile_random_maclaurin_features_s8_kernel(tc, x, w1, w2, c, r, v_words, v_sca
 
         def weave_half(u, h):
             dst, src = weave_views(u)
-            nc.gpsimd.tensor_scalar(out=dst[:, h], in0=src[:, h], scalar1=1.0, scalar2=0.0, op0=MULT, op1=ADD)
+            pool_copy(dst[:, h], src[:, h])
 
         def weave_quarter(copy, u, t):
             dst, src = weave_views(u)
             copy(out=dst[:, t // 2, t % 2], in_=src[:, t // 2, t % 2])
-
-        def quantize_feat(u, lo, hi):
-            f, g = UNITS[u]
-            if ("zf", f, g) not in mx:
-                mx["zf", f, g] = mx_tiles("zf%d%d" % (f, g))
-            quantize(mx["zf", f, g], slice(lo * P, hi * P), z_feat[u][:, lo * PASS : hi * PASS])
-            for t in range(lo, hi):
-                fresh.append((clock[0], ("zf", f, g, t)))
 
         def turn(u, pair):
             turned[u, pair] = bank("turn%d" % pair)
@@ -298,31 +266,61 @@ def tile_random_maclaurin_features_s8_kernel(tc, x, w1, w2, c, r, v_words, v_sca
             for n in range(4):
                 nc.tensor.transpose(turned[u, pair][:, quarter(n)], words[:, quarter(4 * pair + n)], ident[:])
 
-        def copy_turned(copy, u, pair):
+        def copy_turned(u, pair):
             if u not in z_rows:
                 z_rows[u] = ring.tile([P, 4 * PASS], BF16, name="z_rows", tag="z_rows", bufs=3, align_bytes=64)
-            copy(
+            nc.scalar.copy(
                 out=z_rows[u][:].bitcast(F32)[:, pair * PASS : (pair + 1) * PASS].rearrange("m (s p h) -> m s p h", s=2, h=2),
                 in_=turned[u, pair][:].rearrange("m (s h p) -> m s p h", s=2, h=2),
             )
 
-        def quantize_rows(u, lo, hi):
+        def quantize_z(kind, u, lo, hi, step):
             f, g = UNITS[u]
-            if ("zr", f, g) not in mx:
-                mx["zr", f, g] = mx_tiles("zr%d%d" % (f, g))
-            quantize(mx["zr", f, g], slice(lo * P, hi * P), z_rows[u][:, lo * PASS : hi * PASS])
-            for s in range(lo, hi):
-                fresh.append((clock[0], ("zr", f, g, s)))
+            if (kind, f, g) not in mx:
+                mx[kind, f, g] = mx_tiles("%s%d%d" % (kind, f, g))
+            src = z_feat[u] if kind == "zf" else z_rows[u]
+            quantize(mx[kind, f, g], slice(lo * P, hi * P), src[:, lo * PASS : hi * PASS])
+            fresh.extend([(step, (kind, f, g, n)) for n in range(lo, hi)])
+
+        z_due = []
+        weave_due = []
+        for u in range(LAST):
+            f, g = UNITS[u]
+            after = STEPS * (u + 1)
+            if u in ROWS_SOON:
+                z_due.append((after + ROWS_SOON[u], "zr", u, 0, 4))
+            elif u < HALF:
+                z_due.append((after + QUIET, "zr", u, 0, 4))
+            else:
+                z_due.append((min(after + 2 * STEPS - 1, n_steps - LAG), "zr", u, 0, 4))
+        for u in range(LAST):
+            f, g = UNITS[u]
+            after = STEPS * (u + 1)
+            pool_quarters = 2 * POOL_HALVES.get(u, 0)
+            if f == 3:
+                weave_due.extend([(after + t // 2, u, t) for t in range(4)])
+                z_due.extend([(after + n + LAG, "zf", u, 2 * n, 2 * n + 2) for n in range(2)])
+            elif pool_quarters == 0:
+                weave_due.extend([(after + 4 + 2 * t, u, t) for t in range(4)])
+            elif pool_quarters == 2:
+                weave_due.extend([(after + t, u, t) for t in (2, 3)])
+                z_due.append((after + 3 + LAG, "zf", u, 0, 4))
+            elif f == 2:
+                z_due.append((after + QUIET, "zf", u, 0, 4))
+            if f < 2:
+                z_due.append((STEPS * (HALF + 2 * g) + PARKED[f], "zf", u, 0, 4))
+        z_due.append((n_steps - 1, "zr", LAST, 0, 2))
 
         pred_rows = out_0.rearrange("(g m t) n -> g t m n", g=2, t=4)
         moment_rows = out_1.rearrange("(f m s) n -> f s m n", f=4, s=4)
-        free_banks = ["out%d" % b for b in range(OUT_BANKS)]
-        finished = []
-        running = []
-        lent = []
-        clock = [0]
-        moments = [(moment_rows[f, i], [("zr", f, g, i) for g in range(2)]) for f in range(4) for i in range(4)]
+        moments = [(moment_rows[f, s], [("zr", f, g, s) for g in range(2)]) for f in range(4) for s in range(4)]
         preds = [(pred_rows[g, t], [("zf", f, g, t) for f in range(4)]) for g in range(2) for t in range(4)]
+        free_banks = ["out0", "out1"]
+        lent_banks = []
+        running = []
+        finished = []
+        preds_from = STEPS * first_unit_with(3)
+        held_groups = 3
 
         def open_group(banks, waiting):
             tag = take(banks)
@@ -331,159 +329,158 @@ def tile_random_maclaurin_features_s8_kernel(tc, x, w1, w2, c, r, v_words, v_sca
             running.append(group)
             return group
 
-        def pick():
+        def pick(step):
             for group in running:
                 if group["passes"][-1] in usable:
                     return group
-            if moments and lent and moments[0][1][0] in usable:
-                return open_group(lent, moments)
+            if moments and lent_banks and moments[0][1][0] in usable:
+                return open_group(lent_banks, moments)
             if moments and free_banks and moments[0][1][-1] in usable:
                 return open_group(free_banks, moments)
             for group in running:
                 if group["passes"][group["done"]] in usable:
                     return group
-            if preds and clock[0] >= PRED_FROM and free_banks and preds[0][1][0] in usable and (len(running) < HOLD or preds[0][1][-1] in usable):
-                return open_group(free_banks, preds)
+            if preds and step >= preds_from and free_banks and preds[0][1][0] in usable:
+                if len(running) < held_groups or preds[0][1][-1] in usable:
+                    return open_group(free_banks, preds)
             if moments and free_banks and not preds and moments[0][1][0] in usable:
                 return open_group(free_banks, moments)
             return None
 
-        def one_pass():
-            group = pick()
+        def one_pass(step):
+            group = pick(step)
             if group is None:
                 return
             n = group["done"]
             total = len(group["passes"])
             kind, f, g, i = group["passes"][n]
             if kind == "zf":
-                rhs = (v_codes[:, f, :].bitcast(FP4X4), v_plane[:, f * C : (f + 1) * C])
+                rhs = (v_codes[:, f, :].bitcast(FP4X4), v_scale_sb[:, f * C : (f + 1) * C])
             else:
                 rhs = operand(mx["y", g, 0], whole)
             matmul(group["tile"][:], operand(mx[kind, f, g], quarter(i)), rhs, n == 0, n == total - 1)
             group["done"] = n + 1
             if n == total - 1:
-                finished.append((group["tag"], group["tile"], group["dram"]))
+                finished.append(group)
                 running[:] = [other for other in running if other["tag"] != group["tag"]]
 
-        def run_passes(count):
-            while fresh and (not open_units or fresh[0][0] <= clock[0] - AGE):
+        def run_passes(count, step):
+            while fresh and (step == n_steps or fresh[0][0] <= step - LAG):
                 usable.add(take(fresh)[1])
-            for step in range(count):
-                one_pass()
+            for n in range(count):
+                one_pass(step)
 
-        def drain(copy):
-            tag, tile, dram = take(finished)
-            result = ring.tile([P, PASS], F32, name="result", tag="result", bufs=RESULT_BUFS)
-            copy(out=result[:], in_=tile[:])
-            nc.sync.dma_start(out=dram, in_=result[:])
-            if tag[0] != "t" or not open_units:
-                free_banks.append(tag)
+        def drain(copy, step):
+            group = take(finished)
+            result = ring.tile([P, PASS], F32, name="result", tag="result", bufs=8)
+            copy(out=result[:], in_=group["tile"][:])
+            nc.sync.dma_start(out=group["dram"], in_=result[:])
+            if step == n_steps or not group["tag"].startswith("turn"):
+                free_banks.append(group["tag"])
 
-        open_units = [1]
-        for j in range(2):
-            fill(j)
-        for j in range(n_slots):
-            u, i = divmod(j, 8)
-            f, g = UNITS[u]
-            clock[0] = j
-            if j > PAIRED_UNTIL:
+        two_runs = [u for u in range(len(UNITS)) if u < HALF or u == LAST]
+        paired_until = STEPS * HALF
+
+        fill(0)
+        fill(1)
+        for j in range(n_steps):
+            u, i = divmod(j, STEPS)
+            before = u - 1
+
+            if j > paired_until:
                 targets = (j + 1, j + 2)
+            elif j % 2:
+                targets = (j + 2, j + 1, j + 4)
             else:
-                targets = (j + 2, j + 1, j + 4) if j % 2 else (j + 3, j + 2)
-            if i == 0 and u > 0 and u - 1 not in SPLIT_UNITS:
-                assert not lent and all(group["tag"][0] != "t" for group in running)
-                turn(u - 1, 0)
-                turn(u - 1, 1)
+                targets = (j + 3, j + 2)
+            if i == 0 and u > 0 and before not in two_runs:
+                turn(before, 0)
+                turn(before, 1)
             for target in targets:
-                if target < n_slots and target not in h_bank and ("w", target % 8 // 4, UNITS[target // 8][0]) in mx and ("x", UNITS[target // 8][1], 0) in mx:
+                if target < n_steps and target not in h_bank and all(key in mx for key in h_operands(target)):
                     fill(target)
-            if i == 0 and u - 1 in SPLIT_UNITS:
-                turn(u - 1, 1)
-            if i == 6 and u in SPLIT_UNITS:
-                assert "turn0" not in lent and all(group["tag"] != "turn0" for group in running)
+            if i == 0 and before in two_runs:
+                turn(before, 1)
+            if i == 6 and u in two_runs:
                 turn(u, 0)
-            if j == X1_SLOT:
-                x_banks = [transpose_x(1, half, "turn%d" % half) for half in range(2)]
-            lent.extend(LEND.get(j, ()))
-            if j >= 10:
-                run_passes((LAST_PASSES if j >= LAST_FROM else LATE_PASSES if j >= LATE_FROM else PASSES_PER_SLOT)[i])
-            closing = u > 0 and UNITS[u - 1][0] == 3
-            turn_at = CLOSE_TURN if closing else (0, 1)
+            if j == x_step:
+                x_banks = [turn_x(1, h) for h in range(2)]
+            if u == LAST and i == 2:
+                lent_banks.extend(["turn0", "turn1"])
+            if u < HALF:
+                run_passes(0 if i == 0 else 1, j)
+            else:
+                run_passes(1 if i in (0, STEPS - 1) else 2, j)
+
             if i == 0:
-                for h in range(POOL_HALVES.get(u - 1, 0)):
-                    weave_half(u - 1, h)
-            consume(j)
-            if j == PAIRED_UNTIL or len(h_bank) + len(h_free) >= n_slots:
+                for h in range(POOL_HALVES.get(before, 0)):
+                    weave_half(before, h)
+            if j == x_step + 1:
+                for n in range(POOL_Y):
+                    pool_copy(
+                        stage(("y", 0, 0))[:].rearrange("p (n j) -> p n j", j=4)[:, quarter(n)],
+                        loaded["y", 0, 0][:].rearrange("p j n -> p n j")[:, quarter(n)],
+                    )
+
+            multiply(j)
+            if j == paired_until or len(h_bank) + len(h_free) >= n_steps:
                 free_banks.append(h_tag[j])
             else:
                 h_free.append(h_tag[j])
-            for due, key in to_quantize:
-                if due == j:
+            for key in input_due:
+                if input_due[key] == j:
                     quantize_staged(key)
-            for early in ROWS_DUE:
-                if ROWS_DUE[early] == j:
-                    quantize_rows(early, 0, 4)
-            if i == 7 and u == last_unit:
-                quantize_rows(u, 0, 2)
-            if j in CLOSE_DUE:
-                step = 4 // len(CLOSE_DUE)
-                n = CLOSE_DUE.index(j)
-                quantize_feat(u - 1, n * step, (n + 1) * step)
-            for early in FEAT_DUE:
-                if FEAT_DUE[early] == j:
-                    quantize_feat(early, 0, 4)
-            if j == X1_SLOT:
-                for half in range(2):
-                    copy_x(1, half, x_banks[half])
-            if j == R1_SLOT:
-                spread_r(1)
-            if i == 0 and u - 1 in SPLIT_UNITS:
-                copy_turned(nc.scalar.copy, u - 1, 1)
-            if u > 0 and i in turn_at and u - 1 not in SPLIT_UNITS:
-                copy_turned(nc.scalar.copy, u - 1, turn_at.index(i))
-            if i == 6 and u in SPLIT_UNITS:
-                copy_turned(nc.scalar.copy, u, 0)
-            for early in SCALAR_WEAVE:
-                for t, due in enumerate(SCALAR_WEAVE[early]):
-                    if j and due == j:
-                        weave_quarter(nc.scalar.copy, early, t)
-            budget = (FIRST_PIECES if u == 0 else PIECES_PER_SLOT)[i]
-            while finished:
-                drain(nc.scalar.copy)
-                budget = budget - 1
-            for n in range(budget):
-                if pieces:
-                    key, piece = take(pieces)
-                    interleave(nc.scalar.copy, key, piece, piece + 1)
-                    if piece == 3:
-                        assert DUE[key] > j
-                        to_quantize.append((DUE[key], key))
+            for due, kind, unit, lo, hi in z_due:
+                if due == j:
+                    quantize_z(kind, unit, lo, hi, j)
 
-        open_units.clear()
-        clock[0] = 2 * n_slots
-        free_banks.append("turn0")
-        assert not lent and all(group["tag"] != "turn1" for group in running)
-        turn(last_unit, 1)
-        copy_turned(nc.scalar.copy, last_unit, 1)
-        free_banks.append("turn1")
-        run_passes(TAIL[0])
-        weave_quarter(nc.vector.tensor_copy, last_unit, 0)
-        weave_quarter(nc.vector.tensor_copy, last_unit, 1)
-        quantize_feat(last_unit, 0, 1)
-        weave_quarter(nc.vector.tensor_copy, last_unit, 2)
-        quantize_feat(last_unit, 1, 2)
-        while finished:
-            drain(nc.scalar.copy)
-        run_passes(TAIL[1])
-        weave_quarter(nc.vector.tensor_copy, last_unit, 3)
-        quantize_feat(last_unit, 2, 3)
-        quantize_rows(last_unit, 2, 4)
-        quantize_feat(last_unit, 3, 4)
-        while finished:
-            drain(nc.scalar.copy)
-        turn_of = 0
-        while moments or preds or running or finished:
-            run_passes(2)
+            if j == x_step:
+                for h in range(2):
+                    copy_x(1, h, x_banks[h])
+            if j == x_step + LAG:
+                spread_r(1)
+            if i == 0 and before in two_runs:
+                copy_turned(before, 1)
+            if u > 0 and before not in two_runs:
+                first = 4 if UNITS[before][0] == 3 else 0
+                if i in (first, first + 1):
+                    copy_turned(before, i - first)
+            if i == 6 and u in two_runs:
+                copy_turned(u, 0)
+            for due, unit, t in weave_due:
+                if due == j:
+                    weave_quarter(nc.scalar.copy, unit, t)
+            share = 2 if j == 0 else 0 if j == x_step or i == 0 else 1
             while finished:
-                drain((nc.vector.tensor_copy, nc.scalar.copy)[turn_of % 2])
-                turn_of = turn_of + 1
+                drain(nc.scalar.copy, j)
+                share = share - 1
+            for n in range(min(share, len(scalar_quarters))):
+                key, part = take(scalar_quarters)
+                assert input_due[key] > j
+                interleave(nc.scalar.copy, key, part, part + 1)
+
+        free_banks.append("turn0")
+        turn(LAST, 1)
+        copy_turned(LAST, 1)
+        free_banks.append("turn1")
+        run_passes(ENDING_PASSES, n_steps)
+        weave_quarter(nc.vector.tensor_copy, LAST, 0)
+        weave_quarter(nc.vector.tensor_copy, LAST, 1)
+        quantize_z("zf", LAST, 0, 1, n_steps)
+        weave_quarter(nc.vector.tensor_copy, LAST, 2)
+        quantize_z("zf", LAST, 1, 2, n_steps)
+        while finished:
+            drain(nc.scalar.copy, n_steps)
+        run_passes(ENDING_PASSES, n_steps)
+        weave_quarter(nc.vector.tensor_copy, LAST, 3)
+        quantize_z("zf", LAST, 2, 3, n_steps)
+        quantize_z("zr", LAST, 2, 4, n_steps)
+        quantize_z("zf", LAST, 3, 4, n_steps)
+        while finished:
+            drain(nc.scalar.copy, n_steps)
+        drained = 0
+        while moments or preds or running:
+            run_passes(2, n_steps)
+            while finished:
+                drain((nc.vector.tensor_copy, nc.scalar.copy)[drained % 2], n_steps)
+                drained = drained + 1

from contextlib import ExitStack

import concourse.mybir as mybir
from concourse.masks import make_identity

M, K, D, C, R = 1024, 512, 2048, 512, 512
FLOPS = 2 * (2 * M * K * D + M * D * C + M * D * R)

F32 = mybir.dt.float32
BF16 = mybir.dt.bfloat16
U32 = mybir.dt.uint32
I32 = mybir.dt.int32
U8 = mybir.dt.uint8
FP8X4 = mybir.dt.float8_e4m3fn_x4
FP4X4 = mybir.dt.float4_e2m1fn_x4
MULT = mybir.AluOpType.mult
ADD = mybir.AluOpType.add

P = 128
PASS = 512
STEPS = 8

UNITS = [(0, 0), (0, 1), (1, 0), (1, 1), (2, 0), (3, 0), (2, 1), (3, 1)]
HALF = len(UNITS) // 2
LAST = len(UNITS) - 1

LAG = 2
QUIET = 6
POOL_HALVES = {0: 2, 1: 2, 2: 2, 4: 2, 6: 1}
ROWS_SOON = {3: 3, 6: 2}
PARKED = (1, QUIET)
POOL_Y = 2
ENDING_PASSES = 4


def take(queue):
    first = queue[0]
    queue[:] = queue[1:]
    return first


def quarter(i):
    return slice(i * P, (i + 1) * P)


def first_unit_with(f):
    return min(u for u in range(len(UNITS)) if UNITS[u][0] == f)


def tile_random_maclaurin_features_s8_kernel(tc, x, w1, w2, c, r, v_words, v_scales, y, out_0, out_1):
    nc = tc.nc
    n_steps = STEPS * len(UNITS)
    whole = slice(0, PASS)
    halves = (slice(0, PASS // 2), slice(PASS // 2, PASS))

    with ExitStack() as ctx:
        keep = ctx.enter_context(tc.tile_pool(name="keep", bufs=1))
        ring = ctx.enter_context(tc.tile_pool(name="ring", bufs=2))
        psum = ctx.enter_context(tc.psum_pool(name="psum", bufs=1))
        ctx.enter_context(tc.manual_schedule())

        def bank(tag):
            return psum.tile([P, PASS], F32, name=tag, tag=tag)

        def mx_tiles(name):
            codes = keep.tile([P, PASS], U32, name=name + "_codes", align_bytes=64)
            scales = keep.tile([P, PASS], U8, name=name + "_scales", align_bytes=64)
            return codes, scales

        def quantize(tiles, cols, src):
            nc.vector.quantize_mx(out=tiles[0][:, cols].bitcast(FP8X4), scales=tiles[1][:, cols], in_=src)

        def operand(tiles, cols):
            return tiles[0][:, cols].bitcast(FP8X4), tiles[1][:, cols]

        def matmul(out, lhs, rhs, start, stop):
            nc.tensor.matmul_mx(out=out, lhsT=lhs[0], lhsT_scale=lhs[1], rhs=rhs[0], rhs_scale=rhs[1], start=start, stop=stop)

        def pool_copy(out, in_):
            nc.gpsimd.tensor_scalar(out=out, in0=in_, scalar1=1.0, scalar2=0.0, op0=MULT, op1=ADD)

        r_sb = keep.tile([P, 8], BF16, name="r_sb")
        nc.scalar.dma_start(out=r_sb[:].rearrange("m (g t) -> m g t", g=2), in_=r.rearrange("(g m t) -> m g t", g=2, t=4))
        c_sb = keep.tile([P, 16], BF16, name="c_sb")
        nc.scalar.dma_start(out=c_sb[:].rearrange("m (f s) -> m f s", f=4), in_=c.rearrange("(f m s) -> m f s", f=4, s=4))

        ident = keep.tile([P, P], F32, name="ident")
        make_identity(nc, ident[:])
        v_scale_sb = keep.tile([P, 4 * C], U8, name="v_scale_sb", align_bytes=64)
        nc.gpsimd.memset(v_scale_sb[:].bitcast(I32), 0)

        loaded = {}
        x_rows = x.rearrange("(g m t) k -> g m (t k)", g=2, t=4)
        w_rows = [w.rearrange("(p j) d -> p j d", j=4) for w in (w1, w2)]
        y_rows = y.rearrange("(g p j) n -> g p j n", g=2, j=4)

        def load_x(g):
            for h in range(2):
                tile = keep.tile([P, 2 * K], BF16, name="x_in%d%d" % (g, h))
                nc.sync.dma_start(out=tile[:], in_=x_rows[g][:, h * 2 * K : (h + 1) * 2 * K])
                loaded["x", g, h] = tile

        def load_k_first(key, src):
            tile = keep.tile([P, 4, src.shape[2]], BF16, name="%s_in%d%d" % key)
            nc.sync.dma_start(out=tile[:], in_=src)
            loaded[key] = tile

        def load_w(n, f):
            load_k_first(("w", n, f), w_rows[n][:, :, f * PASS : (f + 1) * PASS])

        load_x(0)
        for n in range(2):
            load_k_first(("w_first", n, 0), w_rows[0][:, :, halves[n]])
        load_w(1, 0)
        load_x(1)
        load_w(0, 1)
        load_k_first(("y", 0, 0), y_rows[0])
        load_w(1, 1)
        load_k_first(("y", 1, 0), y_rows[1])
        for f in (2, 3):
            load_w(0, f)
            load_w(1, f)
        v_codes = keep.tile([P, 4, 2 * C], U8, name="v_codes", align_bytes=64)
        nc.sync.dma_start(out=v_codes[:].bitcast(I32), in_=v_words.bitcast(I32).rearrange("f p n -> p f n"))
        for q in range(4):
            nc.sync.dma_start(
                out=v_scale_sb[:].bitcast(I32)[32 * q : 32 * q + 4, :].rearrange("p (f n) -> p f n", f=4),
                in_=v_scales.bitcast(I32)[:, 4 * q : 4 * q + 4, :].rearrange("f p n -> p f n"),
            )

        staged = {}
        mx = {}

        def stage(key):
            if key not in staged:
                staged[key] = ring.tile([P, 4 * PASS], BF16, name="stage", tag="stage", bufs=6, align_bytes=64)
            return staged[key]

        def weight_views(key, src):
            return (
                stage(key)[:].rearrange("p (s a b j) -> p a s b j", s=4, b=2, j=4),
                src[:].rearrange("p j (a b s) -> p a s b j", b=2, s=4),
            )

        def interleave(copy, key, lo, hi):
            if key[0] == "w":
                dst, src = weight_views(key, loaded[key])
                copy(out=dst[:, 16 * lo : 16 * hi], in_=src[:, 16 * lo : 16 * hi])
            else:
                copy(
                    out=stage(key)[:].rearrange("p (a i j) -> p a j i", i=4, j=4)[:, 32 * lo : 32 * hi],
                    in_=loaded[key][:].rearrange("p j (a i) -> p a j i", i=4)[:, 32 * lo : 32 * hi],
                )

        def quantize_staged(key):
            mx[key] = mx_tiles("%s%d%d" % key)
            quantize(mx[key], whole, staged[key][:])

        def turn_x(g, h):
            dst = bank("turn%d" % h)
            words = loaded["x", g, h][:].bitcast(F32)
            for e in range(2):
                for u in range(2):
                    nc.tensor.transpose(dst[:, quarter(2 * e + u)], words[:, 256 * e + u : 256 * (e + 1) : 2], ident[:])
            return dst

        def copy_x(g, h, src):
            nc.scalar.copy(
                out=stage(("x", g, 0))[:].bitcast(F32)[:, h * PASS : (h + 1) * PASS].rearrange("p (m e u) -> p m e u", e=2, u=2),
                in_=src[:].rearrange("p (e u m) -> p m e u", e=2, u=2),
            )

        r_words = r_sb[:].bitcast(F32)
        r_all = keep.tile([P, M], BF16, name="r_all")

        def spread_r(g):
            r_bank = bank("out%d" % g)
            for h in range(2):
                word = r_words[:, 2 * g + h : 2 * g + h + 1]
                nc.tensor.transpose(r_bank[:, quarter(h)], word.to_broadcast([P, P]), ident[:])
            nc.scalar.copy(out=r_all[:, g * PASS : (g + 1) * PASS], in_=r_bank[:, 0 : 2 * P].bitcast(BF16))

        spread_r(0)
        x_banks = [turn_x(0, h) for h in range(2)]
        for h in range(2):
            copy_x(0, h, x_banks[h])
        for n in range(2):
            dst, src = weight_views(("w", 0, 0), loaded["w_first", n, 0])
            nc.vector.tensor_copy(out=dst[:, 32 * n : 32 * n + 32], in_=src)
        mx["x", 0, 0] = mx_tiles("x00")
        quantize(mx["x", 0, 0], halves[0], staged["x", 0, 0][:, 0 : 2 * PASS])
        quantize_staged(("w", 0, 0))
        quantize(mx["x", 0, 0], halves[1], staged["x", 0, 0][:, 2 * PASS : 4 * PASS])
        interleave(nc.vector.tensor_copy, ("w", 1, 0), 0, 2)
        interleave(nc.scalar.copy, ("w", 1, 0), 2, 4)

        x_step = 1
        input_due = {("w", 1, 0): 1, ("x", 1, 0): x_step + 1 + LAG}
        for f in (1, 2):
            for n in range(2):
                input_due["w", n, f] = STEPS * (first_unit_with(f) - 1) + QUIET
            if f == 1:
                for g in range(2):
                    input_due["y", g, 0] = STEPS * 2 + QUIET
        input_due["w", 0, 3] = STEPS * first_unit_with(3) - 2 - LAG
        input_due["w", 1, 3] = STEPS * first_unit_with(3) - 1
        later_inputs = [key for key in input_due if key[0] == "y" or key[2] > 0]
        scalar_quarters = [(key, i) for key in later_inputs for i in range(POOL_Y if key == ("y", 0, 0) else 0, 4)]

        h_free = ["h%d" % b for b in range(4)]
        h_tag = {}
        h_bank = {}
        scaled = {}
        z_plain = {}
        z_feat = {}
        z_rows = {}
        turned = {}
        fresh = []
        usable = set()

        def h_operands(j):
            f, g = UNITS[j // STEPS]
            return ("w", j % STEPS // 4, f), ("x", g, 0)

        def fill(j):
            weight, rows = h_operands(j)
            h_tag[j] = take(h_free)
            h_bank[j] = bank(h_tag[j])
            for cols in halves if j == 0 else (whole,):
                matmul(h_bank[j][:, cols], operand(mx[weight], quarter(j % 4)), operand(mx[rows], cols), True, True)

        def multiply(j):
            u, i = divmod(j, STEPS)
            f, g = UNITS[u]
            s = i % 4
            if i < 4:
                scaled[s] = ring.tile([P, PASS], F32, name="scaled", tag="scaled", bufs=5)
                nc.vector.scalar_tensor_tensor(
                    out=scaled[s][:], in0=h_bank[j][:], scalar=c_sb[:, 4 * f + s : 4 * f + s + 1],
                    in1=r_all[:, g * PASS : (g + 1) * PASS], op0=MULT, op1=MULT,
                )
            else:
                if s == 0:
                    z_plain[u] = ring.tile([P, 4 * PASS], BF16, name="z_plain", tag="z_plain", bufs=3)
                nc.vector.tensor_tensor(out=z_plain[u][:, s * PASS : (s + 1) * PASS], in0=h_bank[j][:], in1=scaled[s][:], op=MULT)

        def weave_views(u):
            if u not in z_feat:
                z_feat[u] = ring.tile([P, 4 * PASS], BF16, name="z_feat", tag="z_feat", bufs=5, align_bytes=64)
            return (
                z_feat[u][:].rearrange("p (h e m s) -> p h e m s", h=2, e=2, s=4),
                z_plain[u][:].rearrange("p (s h m e) -> p h e m s", s=4, h=2, e=2),
            )

        def weave_half(u, h):
            dst, src = weave_views(u)
            pool_copy(dst[:, h], src[:, h])

        def weave_quarter(copy, u, t):
            dst, src = weave_views(u)
            copy(out=dst[:, t // 2, t % 2], in_=src[:, t // 2, t % 2])

        def turn(u, pair):
            turned[u, pair] = bank("turn%d" % pair)
            words = z_plain[u][:].bitcast(F32)
            for n in range(4):
                nc.tensor.transpose(turned[u, pair][:, quarter(n)], words[:, quarter(4 * pair + n)], ident[:])

        def copy_turned(u, pair):
            if u not in z_rows:
                z_rows[u] = ring.tile([P, 4 * PASS], BF16, name="z_rows", tag="z_rows", bufs=3, align_bytes=64)
            nc.scalar.copy(
                out=z_rows[u][:].bitcast(F32)[:, pair * PASS : (pair + 1) * PASS].rearrange("m (s p h) -> m s p h", s=2, h=2),
                in_=turned[u, pair][:].rearrange("m (s h p) -> m s p h", s=2, h=2),
            )

        def quantize_z(kind, u, lo, hi, step):
            f, g = UNITS[u]
            if (kind, f, g) not in mx:
                mx[kind, f, g] = mx_tiles("%s%d%d" % (kind, f, g))
            src = z_feat[u] if kind == "zf" else z_rows[u]
            quantize(mx[kind, f, g], slice(lo * P, hi * P), src[:, lo * PASS : hi * PASS])
            fresh.extend([(step, (kind, f, g, n)) for n in range(lo, hi)])

        z_due = []
        weave_due = []
        for u in range(LAST):
            f, g = UNITS[u]
            after = STEPS * (u + 1)
            if u in ROWS_SOON:
                z_due.append((after + ROWS_SOON[u], "zr", u, 0, 4))
            elif u < HALF:
                z_due.append((after + QUIET, "zr", u, 0, 4))
            else:
                z_due.append((min(after + 2 * STEPS - 1, n_steps - LAG), "zr", u, 0, 4))
        for u in range(LAST):
            f, g = UNITS[u]
            after = STEPS * (u + 1)
            pool_quarters = 2 * POOL_HALVES.get(u, 0)
            if f == 3:
                weave_due.extend([(after + t // 2, u, t) for t in range(4)])
                z_due.extend([(after + n + LAG, "zf", u, 2 * n, 2 * n + 2) for n in range(2)])
            elif pool_quarters == 0:
                weave_due.extend([(after + 4 + 2 * t, u, t) for t in range(4)])
            elif pool_quarters == 2:
                weave_due.extend([(after + t, u, t) for t in (2, 3)])
                z_due.append((after + 3 + LAG, "zf", u, 0, 4))
            elif f == 2:
                z_due.append((after + QUIET, "zf", u, 0, 4))
            if f < 2:
                z_due.append((STEPS * (HALF + 2 * g) + PARKED[f], "zf", u, 0, 4))
        z_due.append((n_steps - 1, "zr", LAST, 0, 2))

        pred_rows = out_0.rearrange("(g m t) n -> g t m n", g=2, t=4)
        moment_rows = out_1.rearrange("(f m s) n -> f s m n", f=4, s=4)
        moments = [(moment_rows[f, s], [("zr", f, g, s) for g in range(2)]) for f in range(4) for s in range(4)]
        preds = [(pred_rows[g, t], [("zf", f, g, t) for f in range(4)]) for g in range(2) for t in range(4)]
        free_banks = ["out0", "out1"]
        lent_banks = []
        running = []
        finished = []
        preds_from = STEPS * first_unit_with(3)
        held_groups = 3

        def open_group(banks, waiting):
            tag = take(banks)
            dram, passes = take(waiting)
            group = dict(tag=tag, tile=bank(tag), dram=dram, passes=passes, done=0)
            running.append(group)
            return group

        def pick(step):
            for group in running:
                if group["passes"][-1] in usable:
                    return group
            if moments and lent_banks and moments[0][1][0] in usable:
                return open_group(lent_banks, moments)
            if moments and free_banks and moments[0][1][-1] in usable:
                return open_group(free_banks, moments)
            for group in running:
                if group["passes"][group["done"]] in usable:
                    return group
            if preds and step >= preds_from and free_banks and preds[0][1][0] in usable:
                if len(running) < held_groups or preds[0][1][-1] in usable:
                    return open_group(free_banks, preds)
            if moments and free_banks and not preds and moments[0][1][0] in usable:
                return open_group(free_banks, moments)
            return None

        def one_pass(step):
            group = pick(step)
            if group is None:
                return
            n = group["done"]
            total = len(group["passes"])
            kind, f, g, i = group["passes"][n]
            if kind == "zf":
                rhs = (v_codes[:, f, :].bitcast(FP4X4), v_scale_sb[:, f * C : (f + 1) * C])
            else:
                rhs = operand(mx["y", g, 0], whole)
            matmul(group["tile"][:], operand(mx[kind, f, g], quarter(i)), rhs, n == 0, n == total - 1)
            group["done"] = n + 1
            if n == total - 1:
                finished.append(group)
                running[:] = [other for other in running if other["tag"] != group["tag"]]

        def run_passes(count, step):
            while fresh and (step == n_steps or fresh[0][0] <= step - LAG):
                usable.add(take(fresh)[1])
            for n in range(count):
                one_pass(step)

        def drain(copy, step):
            group = take(finished)
            result = ring.tile([P, PASS], F32, name="result", tag="result", bufs=8)
            copy(out=result[:], in_=group["tile"][:])
            nc.sync.dma_start(out=group["dram"], in_=result[:])
            if step == n_steps or not group["tag"].startswith("turn"):
                free_banks.append(group["tag"])

        two_runs = [u for u in range(len(UNITS)) if u < HALF or u == LAST]
        paired_until = STEPS * HALF

        fill(0)
        fill(1)
        for j in range(n_steps):
            u, i = divmod(j, STEPS)
            before = u - 1

            if j > paired_until:
                targets = (j + 1, j + 2)
            elif j % 2:
                targets = (j + 2, j + 1, j + 4)
            else:
                targets = (j + 3, j + 2)
            if i == 0 and u > 0 and before not in two_runs:
                turn(before, 0)
                turn(before, 1)
            for target in targets:
                if target < n_steps and target not in h_bank and all(key in mx for key in h_operands(target)):
                    fill(target)
            if i == 0 and before in two_runs:
                turn(before, 1)
            if i == 6 and u in two_runs:
                turn(u, 0)
            if j == x_step:
                x_banks = [turn_x(1, h) for h in range(2)]
            if u == LAST and i == 2:
                lent_banks.extend(["turn0", "turn1"])
            if u < HALF:
                run_passes(0 if i == 0 else 1, j)
            else:
                run_passes(1 if i in (0, STEPS - 1) else 2, j)

            if i == 0:
                for h in range(POOL_HALVES.get(before, 0)):
                    weave_half(before, h)
            if j == x_step + 1:
                for n in range(POOL_Y):
                    pool_copy(
                        stage(("y", 0, 0))[:].rearrange("p (n j) -> p n j", j=4)[:, quarter(n)],
                        loaded["y", 0, 0][:].rearrange("p j n -> p n j")[:, quarter(n)],
                    )

            multiply(j)
            if j == paired_until or len(h_bank) + len(h_free) >= n_steps:
                free_banks.append(h_tag[j])
            else:
                h_free.append(h_tag[j])
            for key in input_due:
                if input_due[key] == j:
                    quantize_staged(key)
            for due, kind, unit, lo, hi in z_due:
                if due == j:
                    quantize_z(kind, unit, lo, hi, j)

            if j == x_step:
                for h in range(2):
                    copy_x(1, h, x_banks[h])
            if j == x_step + LAG:
                spread_r(1)
            if i == 0 and before in two_runs:
                copy_turned(before, 1)
            if u > 0 and before not in two_runs:
                first = 4 if UNITS[before][0] == 3 else 0
                if i in (first, first + 1):
                    copy_turned(before, i - first)
            if i == 6 and u in two_runs:
                copy_turned(u, 0)
            for due, unit, t in weave_due:
                if due == j:
                    weave_quarter(nc.scalar.copy, unit, t)
            share = 2 if j == 0 else 0 if j == x_step or i == 0 else 1
            while finished:
                drain(nc.scalar.copy, j)
                share = share - 1
            for n in range(min(share, len(scalar_quarters))):
                key, part = take(scalar_quarters)
                assert input_due[key] > j
                interleave(nc.scalar.copy, key, part, part + 1)

        free_banks.append("turn0")
        turn(LAST, 1)
        copy_turned(LAST, 1)
        free_banks.append("turn1")
        run_passes(ENDING_PASSES, n_steps)
        weave_quarter(nc.vector.tensor_copy, LAST, 0)
        weave_quarter(nc.vector.tensor_copy, LAST, 1)
        quantize_z("zf", LAST, 0, 1, n_steps)
        weave_quarter(nc.vector.tensor_copy, LAST, 2)
        quantize_z("zf", LAST, 1, 2, n_steps)
        while finished:
            drain(nc.scalar.copy, n_steps)
        run_passes(ENDING_PASSES, n_steps)
        weave_quarter(nc.vector.tensor_copy, LAST, 3)
        quantize_z("zf", LAST, 2, 3, n_steps)
        quantize_z("zr", LAST, 2, 4, n_steps)
        quantize_z("zf", LAST, 3, 4, n_steps)
        while finished:
            drain(nc.scalar.copy, n_steps)
        drained = 0
        while moments or preds or running:
            run_passes(2, n_steps)
            while finished:
                drain((nc.vector.tensor_copy, nc.scalar.copy)[drained % 2], n_steps)
                drained = drained + 1
